import numpy as np
import ml_dtypes


def mxq(x, axis, fmt="e4m3"):
    dtype, down = {"e4m3": (ml_dtypes.float8_e4m3fn, 7), "e5m2": (ml_dtypes.float8_e5m2, 14)}[fmt]
    v = np.moveaxis(np.asarray(x, np.float32).astype(ml_dtypes.bfloat16).astype(np.float64), axis, -1)
    blocks = v.reshape(v.shape[:-1] + (-1, 32))
    amax = np.abs(blocks).max(-1, keepdims=True)
    byte = np.maximum(np.where(amax > 0, np.frexp(amax)[1] - 1 + 127, 0) - down, 1)
    scale = np.exp2(byte - 127.0)
    codes = (blocks / scale).astype(np.float32).astype(dtype).astype(np.float64)
    return np.moveaxis((codes * scale).reshape(v.shape), -1, axis)


WIDE = False


def mx_kscale(k):
    if not WIDE:
        return np.ones(k)
    levels = np.array([10, -10, 5, -5, 0])
    if k % 512:
        return np.exp2(np.random.permutation(np.resize(levels, k // 32))).repeat(32)
    a = np.empty((k // 512, 16))
    for p in range(k // 512):
        a[p, :8] = np.random.permutation(np.resize(levels, 8))
        for g in range(8):
            far = levels[np.abs(levels - a[p, g]) >= 10]
            a[p, g + 8] = far[np.random.randint(len(far))]
    return np.exp2(a.ravel()).repeat(32)


def f64(x):
    return np.asarray(x).astype(np.float64)


def striped(idx):
    return np.tile(idx.reshape(-1, 16).T, (8, 1)).astype(np.uint16)


def unstriped(offs):
    return offs[:16].T.reshape(-1).astype(np.int64)


def pack_weight(w):
    k, n = w.shape
    w = f64(np.asarray(w, np.float32).astype(ml_dtypes.bfloat16)).reshape(k // 32, 32, n)
    amax = np.abs(w).max(1)
    byte = np.clip(np.where(amax > 0, np.frexp(amax)[1] - 1 + 127 - 7, 1), 1, 254)
    scaled = (w * np.exp2(127.0 - byte)[:, None, :]).reshape(k, n).astype(np.float32)
    words = np.ascontiguousarray(scaled.reshape(k // 512, 128, 4, n).transpose(0, 1, 3, 2)).astype(ml_dtypes.float8_e4m3fn).view(np.uint8)
    return words, np.ascontiguousarray(byte.astype(np.uint8).reshape(k // 512, 16, n))


def unpack_weight(words, scales):
    g, p, n, _ = words.shape
    vals = np.ascontiguousarray(words).view(ml_dtypes.float8_e4m3fn).astype(np.float64) * np.repeat(np.exp2(scales.astype(np.float64) - 127.0), 8, axis=1)[..., None]
    return vals.transpose(0, 1, 3, 2).reshape(g * 512, n)


def planes(y):
    n, m = y.shape
    v = y.astype(np.float32).astype(ml_dtypes.bfloat16).astype(np.float64).reshape(n // 32, 32, m)
    top = np.abs(v).max(1)
    byte = np.clip(np.where(top > 0, np.frexp(top)[1] - 1 + 127 - 7, 1), 1, 254)
    codes = (v * np.exp2(127.0 - byte)[:, None, :]).reshape(n, m).astype(np.float32).astype(ml_dtypes.float8_e4m3fn).view(np.uint8)
    words = codes.reshape(n // 512, 128, 4, m).transpose(0, 1, 3, 2)
    return np.ascontiguousarray(words), np.ascontiguousarray(byte.astype(np.uint8).reshape(n // 512, 16, m))


def gelu(v):
    return 0.5 * v * (1.0 + np.tanh(np.sqrt(2.0 / np.pi) * (v + 0.044715 * v**3)))


K, T, S, H, N = 1024, 1024, 512, 512, 512


def setup_inputs():
    n = np.random.standard_normal
    s = mx_kscale(K)[:, None]
    u = mx_kscale(H)
    packed_xT = pack_weight(n((K, T)) * s)
    packed_w2 = pack_weight(n((H, N)) / np.sqrt(H) / u[:, None])
    return {
        "x_words": packed_xT[0],
        "x_scales": packed_xT[1],
        "mask": (n((N, T))).astype(np.float32),
        "w1": (n((K, H)) / np.sqrt(K) / s * u).astype(np.float32),
        "w2_words": packed_w2[0],
        "w2_scales": packed_w2[1],
        "offs": striped(np.random.permutation(T)[:S]),
    }


def reference(x_words, x_scales, mask, w1, w2_words, w2_scales, offs):
    xq = unpack_weight(x_words, x_scales)[:, unstriped(offs)]
    h = gelu(mxq(f64(w1), 0, "e4m3").T @ xq)
    y = unpack_weight(w2_words, w2_scales).T @ mxq(h, 0, "e4m3")
    out = f64(mask).copy()
    out[:, unstriped(offs)] = y
    out_0 = out
    return (out_0,) + planes(out_0)

@@ -1,0 +1,239 @@
+from contextlib import ExitStack
+
+import concourse.mybir as mybir
+
+K, T, S, H, N = 1024, 1024, 512, 512, 512
+FLOPS = 2 * K * H * S + 2 * H * N * S
+
+F32 = mybir.dt.float32
+BF16 = mybir.dt.bfloat16
+I32 = mybir.dt.int32
+U32 = mybir.dt.uint32
+U16 = mybir.dt.uint16
+U8 = mybir.dt.uint8
+FP8X4 = mybir.dt.float8_e4m3fn_x4
+GELU = mybir.ActivationFunctionType.Gelu_apprx_tanh
+
+P = 128
+PACK = 4
+PASSES = K // (P * PACK)
+QUADS = 4
+CHUNK = 128
+CHUNKS = S // CHUNK
+W1_VECTOR_M = (32, 88)
+LAST_VECTOR_COLS = 640
+HALF = T // 2
+
+
+def tile_picked_zmae_mlpgelu_po_kernel(
+    tc, x_words, x_scales, mask, w1, w2_words, w2_scales, offs, out_0, out_1, out_2
+):
+    nc = tc.nc
+    with ExitStack() as ctx:
+        keep = ctx.enter_context(tc.tile_pool(name="keep", bufs=1))
+        psum = ctx.enter_context(tc.psum_pool(name="psum", bufs=1))
+
+        offsets = keep.tile([P, S // 16], U16, name="offsets")
+
+        def picks(first, count):
+            return offsets[:, first // 16 : (first + count) // 16]
+
+        warm_in = keep.tile([P, 8], F32, name="warm_in")
+        warm_out = keep.tile([P, 8], F32, name="warm_out")
+        x_scale_table = keep.tile([P, T], U8, name="x_scale_table", align_bytes=64)
+        w2_scale_raw = keep.tile([P, N], U8, name="w2_scale_raw", align_bytes=64)
+        x_scale_rows = keep.tile([P, T], U8, name="x_scale_rows", align_bytes=64)
+        nc.vector.memset(w2_scale_raw[:].bitcast(I32), 0)
+        nc.vector.memset(warm_in[:], 0.0)
+        nc.vector.memset(x_scale_table[:].bitcast(I32), 0)
+
+        w1_raw = [keep.tile([P, PACK, H], F32, name=f"w1_raw{g}") for g in range(PASSES)]
+        x_word_table = [keep.tile([P, T], I32, name=f"x_word_table{g}", align_bytes=64) for g in range(PASSES)]
+        w2_word_raw = keep.tile([P, N], I32, name="w2_word_raw", align_bytes=64)
+        windows = [keep.tile([P, T], F32, name=f"window{t}", align_bytes=64) for t in range(PACK)]
+
+        def load_w1(g, pieces):
+            rows = w1[g * 512 : (g + 1) * 512, :].rearrange("(p j) c -> p j c", j=PACK)
+            step = PACK // pieces
+            for j in range(0, PACK, step):
+                nc.sync.dma_start(out=w1_raw[g][:, j : j + step, :], in_=rows[:, j : j + step, :])
+
+        nc.sync.dma_start(offsets[:], offs)
+        for q in range(QUADS):
+            queue = nc.sync if q < 2 else nc.scalar
+            queue.dma_start(
+                out=x_scale_rows[32 * q : 32 * q + 4 * PASSES, :].bitcast(I32),
+                in_=x_scales[:, 4 * q : 4 * q + 4, :].bitcast(I32),
+            )
+        nc.scalar.activation(out=warm_out[:], in_=warm_in[:], func=GELU)
+        load_w1(0, 1)
+        nc.sync.dma_start(out=x_word_table[0][:], in_=x_words[0].rearrange("p c r -> p (c r)").bitcast(I32))
+        for q in range(QUADS):
+            nc.sync.dma_start(
+                out=w2_scale_raw[32 * q : 32 * q + 4, :].bitcast(I32),
+                in_=w2_scales[0, 4 * q : 4 * q + 4, :].bitcast(I32),
+            )
+        load_w1(1, 1)
+        nc.sync.dma_start(out=x_word_table[1][:], in_=x_words[1].rearrange("p c r -> p (c r)").bitcast(I32))
+        nc.sync.dma_start(out=w2_word_raw[:], in_=w2_words[0].rearrange("p c r -> p (c r)").bitcast(I32))
+        mask_rows = mask.rearrange("(p t) c -> t p c", t=PACK)
+        out_rows = out_0.rearrange("(p t) c -> t p c", t=PACK)
+        for t in range(PACK):
+            nc.sync.dma_start(out=windows[t][:], in_=mask_rows[t])
+
+        for q in range(QUADS):
+            live = slice(32 * q, 32 * q + 4 * PASSES)
+            nc.vector.tensor_copy(out=x_scale_table[live, :].bitcast(I32), in_=x_scale_rows[live, :].bitcast(I32))
+        x_scale = keep.tile([P, S], U8, name="x_scale", align_bytes=64)
+        nc.vector.tensor_copy(out=x_scale[:], in_=x_scale_table[:].indirect(offsets[:]))
+
+        w1_codes = [keep.tile([P, H], U32, name=f"w1_codes{g}", align_bytes=64) for g in range(PASSES)]
+        w1_scale = [keep.tile([P, H], U8, name=f"w1_scale{g}", align_bytes=64) for g in range(PASSES)]
+        x_codes = [keep.tile([P, S], U32, name=f"x_codes{g}", align_bytes=64) for g in range(PASSES)]
+        w2_scale = keep.tile([P, N], U8, name="w2_scale", align_bytes=64)
+
+        def gather_words(g, first, count):
+            nc.vector.tensor_copy(
+                out=x_codes[g][:, first : first + count],
+                in_=x_word_table[g][:].bitcast(U32).indirect(picks(first, count)),
+            )
+
+        def quantise_w1(g, grouped, first, count):
+            cols = slice(first, first + count)
+            nc.vector.quantize_mx(
+                out=w1_codes[g][:, cols].bitcast(FP8X4),
+                scales=w1_scale[g][:, cols],
+                in_=grouped[:, PACK * first : PACK * (first + count)],
+            )
+
+        for g in range(PASSES):
+            grouped = keep.tile([P, H * PACK], BF16, name=f"w1_grouped{g}", align_bytes=64)
+            src = w1_raw[g][:].rearrange("p j (m t) -> p m j t", t=PACK)
+            dst = grouped[:].rearrange("p (t m j) -> p m j t", t=PACK, j=PACK)
+            split = W1_VECTOR_M[g]
+            nc.vector.tensor_copy(out=dst[:, :split], in_=src[:, :split])
+            nc.scalar.copy(out=dst[:, split:], in_=src[:, split:])
+            if g == 0:
+                gather_words(0, 0, S)
+                nc.vector.tensor_copy(
+                    out=w2_scale[:].rearrange("p (t m) -> p m t", t=PACK),
+                    in_=w2_scale_raw[:].rearrange("p (m t) -> p m t", t=PACK),
+                )
+                quantise_w1(0, grouped, 0, H)
+            else:
+                quantise_w1(1, grouped, 0, H // 2)
+                gather_words(1, 0, CHUNK)
+                quantise_w1(1, grouped, H // 2, H // 2)
+                gather_words(1, CHUNK, CHUNK)
+                gather_words(1, 2 * CHUNK, 2 * CHUNK)
+
+        h_bf = keep.tile([P, S * PACK], BF16, name="h_bf", align_bytes=64)
+        h_codes = keep.tile([P, S], U32, name="h_codes", align_bytes=64)
+        h_scale = keep.tile([P, S], U8, name="h_scale", align_bytes=64)
+        w2_codes = keep.tile([P, N], I32, name="w2_codes", align_bytes=64)
+        y_sb = [keep.tile([P, S], F32, name=f"y_sb{t}", align_bytes=64) for t in range(PACK)]
+
+        def first_layer(c):
+            cols = slice(c * CHUNK, (c + 1) * CHUNK)
+            h_ps = psum.tile([P, PACK, CHUNK], F32, name=f"h_ps{c}", tag=f"bank{c}")
+            for t in range(PACK):
+                m = slice(t * P, (t + 1) * P)
+                for g in range(PASSES):
+                    nc.tensor.matmul_mx(
+                        out=h_ps[:, t, :],
+                        lhsT=w1_codes[g][:, m].bitcast(FP8X4),
+                        lhsT_scale=w1_scale[g][:, m],
+                        rhs=x_codes[g][:, cols].bitcast(FP8X4),
+                        rhs_scale=x_scale[4 * g :, cols],
+                        start=(g == 0),
+                        stop=(g == PASSES - 1),
+                    )
+            nc.scalar.activation(
+                out=h_bf[:, PACK * c * CHUNK : PACK * (c + 1) * CHUNK].rearrange("p (n t) -> p n t", t=PACK),
+                in_=h_ps[:].rearrange("p t n -> p n t"),
+                func=GELU,
+            )
+
+        def quantise_h(first, count):
+            cols = slice(first, first + count)
+            nc.vector.quantize_mx(
+                out=h_codes[:, cols].bitcast(FP8X4),
+                scales=h_scale[:, cols],
+                in_=h_bf[:, PACK * first : PACK * (first + count)],
+            )
+
+        def second_layer(t, first, count, bank):
+            cols = slice(first, first + count)
+            y_ps = psum.tile([P, count], F32, name=f"y_ps{t}_{first}", tag=f"bank{bank}")
+            m = slice(t * P, (t + 1) * P)
+            nc.tensor.matmul_mx(
+                out=y_ps[:],
+                lhsT=w2_codes[:, m].bitcast(FP8X4),
+                lhsT_scale=w2_scale[:, m],
+                rhs=h_codes[:, cols].bitcast(FP8X4),
+                rhs_scale=h_scale[:, cols],
+                start=True,
+                stop=True,
+            )
+            if t == 0 and first == 0:
+                nc.vector.tensor_copy(out=y_sb[t][:, cols], in_=y_ps[:])
+            else:
+                nc.scalar.copy(out=y_sb[t][:, cols], in_=y_ps[:])
+
+        def scatter(t, first, count):
+            nc.vector.tensor_copy(out=windows[t][:].indirect(picks(first, count)), in_=y_sb[t][:, first : first + count])
+
+        for c in range(CHUNKS - 1):
+            first_layer(c)
+        nc.vector.tensor_copy(
+            out=w2_codes[:].rearrange("p (t m) -> p m t", t=PACK),
+            in_=w2_word_raw[:].rearrange("p (m t) -> p m t", t=PACK),
+        )
+        quantise_h(0, CHUNK)
+        second_layer(0, 0, CHUNK, CHUNKS)
+        first_layer(CHUNKS - 1)
+        quantise_h(CHUNK, CHUNK)
+        second_layer(0, CHUNK, CHUNK, CHUNKS + 1)
+        scatter(0, 0, CHUNK)
+        quantise_h(2 * CHUNK, 2 * CHUNK)
+        second_layer(0, 2 * CHUNK, 2 * CHUNK, CHUNKS + 2)
+        scatter(0, CHUNK, CHUNK)
+        for t in range(1, PACK):
+            second_layer(t, 0, S, t - 1)
+        scatter(0, 2 * CHUNK, 2 * CHUNK)
+
+        rounded = keep.tile([P, T, PACK], BF16, name="rounded", align_bytes=64)
+        for t in range(PACK):
+            if t > 0:
+                scatter(t, 0, S)
+            nc.sync.dma_start(out=out_rows[t], in_=windows[t][:])
+            if t < PACK - 2:
+                nc.scalar.copy(out=rounded[:, :, t], in_=windows[t][:])
+            elif t == PACK - 2:
+                nc.scalar.copy(
+                    out=rounded[:, :LAST_VECTOR_COLS, t:],
+                    in_=windows[t][:, :LAST_VECTOR_COLS].unsqueeze(2).to_broadcast([P, LAST_VECTOR_COLS, 2]),
+                )
+                nc.scalar.copy(out=rounded[:, LAST_VECTOR_COLS:, t], in_=windows[t][:, LAST_VECTOR_COLS:])
+        last = PACK - 1
+        nc.vector.tensor_copy(out=rounded[:, :HALF, last], in_=windows[last][:, :HALF])
+        nc.scalar.copy(out=rounded[:, LAST_VECTOR_COLS:, last], in_=windows[last][:, LAST_VECTOR_COLS:])
+        nc.vector.tensor_copy(out=rounded[:, HALF:LAST_VECTOR_COLS, last], in_=windows[last][:, HALF:LAST_VECTOR_COLS])
+
+        out_codes = keep.tile([P, T], I32, name="out_codes", align_bytes=64)
+        out_scale = keep.tile([P, T], U8, name="out_scale", align_bytes=64)
+        out_words = out_1[0].rearrange("p c r -> p (c r)").bitcast(I32)
+        for first, count in ((0, HALF), (HALF, HALF // 2), (HALF + HALF // 2, HALF // 2)):
+            cols = slice(first, first + count)
+            nc.vector.quantize_mx(
+                out=out_codes[:, cols].bitcast(FP8X4),
+                scales=out_scale[:, cols],
+                in_=rounded[:, cols, :].rearrange("p c t -> p (c t)"),
+            )
+            nc.sync.dma_start(out=out_words[:, cols], in_=out_codes[:, cols])
+        for q in range(QUADS):
+            queue = nc.sync if q % 2 == 0 else nc.scalar
+            queue.dma_start(
+                out=out_2[0, 4 * q : 4 * q + 4, :].bitcast(I32),
+                in_=out_scale[32 * q : 32 * q + 4, :].bitcast(I32),
+            )

@@ -20,7 +20,8 @@ PASSES = K // (P * PACK)
 QUADS = 4
 CHUNK = 128
 CHUNKS = S // CHUNK
-W1_VECTOR_M = (32, 88)
+W1_PIECES = ((0, 0, 512, 320), (1, 0, 256, 0), (1, 256, 256, 256))
+WARM_PASSES = 2
 LAST_VECTOR_COLS = 640
 HALF = T // 2
 
@@ -47,16 +48,16 @@ def tile_picked_zmae_mlpgelu_po_kernel(
         nc.vector.memset(warm_in[:], 0.0)
         nc.vector.memset(x_scale_table[:].bitcast(I32), 0)
 
-        w1_raw = [keep.tile([P, PACK, H], F32, name=f"w1_raw{g}") for g in range(PASSES)]
+        w1_raw = [
+            keep.tile([P, PACK, width], F32, name=f"w1_raw{u}", tag=f"slot{u}", align_bytes=64) for u, (g, first, width, share) in enumerate(W1_PIECES)
+        ]
         x_word_table = [keep.tile([P, T], I32, name=f"x_word_table{g}", align_bytes=64) for g in range(PASSES)]
         w2_word_raw = keep.tile([P, N], I32, name="w2_word_raw", align_bytes=64)
-        windows = [keep.tile([P, T], F32, name=f"window{t}", align_bytes=64) for t in range(PACK)]
 
-        def load_w1(g, pieces):
-            rows = w1[g * 512 : (g + 1) * 512, :].rearrange("(p j) c -> p j c", j=PACK)
-            step = PACK // pieces
-            for j in range(0, PACK, step):
-                nc.sync.dma_start(out=w1_raw[g][:, j : j + step, :], in_=rows[:, j : j + step, :])
+        def load_w1(u):
+            g, first, width, share = W1_PIECES[u]
+            rows = w1[g * 512 : (g + 1) * 512, first : first + width].rearrange("(p j) c -> p j c", j=PACK)
+            nc.sync.dma_start(out=w1_raw[u][:], in_=rows)
 
         nc.sync.dma_start(offsets[:], offs)
         for q in range(QUADS):
@@ -66,20 +67,19 @@ def tile_picked_zmae_mlpgelu_po_kernel(
                 in_=x_scales[:, 4 * q : 4 * q + 4, :].bitcast(I32),
             )
         nc.scalar.activation(out=warm_out[:], in_=warm_in[:], func=GELU)
-        load_w1(0, 1)
         nc.sync.dma_start(out=x_word_table[0][:], in_=x_words[0].rearrange("p c r -> p (c r)").bitcast(I32))
+        load_w1(0)
         for q in range(QUADS):
             nc.sync.dma_start(
                 out=w2_scale_raw[32 * q : 32 * q + 4, :].bitcast(I32),
                 in_=w2_scales[0, 4 * q : 4 * q + 4, :].bitcast(I32),
             )
-        load_w1(1, 1)
+        load_w1(1)
+        load_w1(2)
         nc.sync.dma_start(out=x_word_table[1][:], in_=x_words[1].rearrange("p c r -> p (c r)").bitcast(I32))
         nc.sync.dma_start(out=w2_word_raw[:], in_=w2_words[0].rearrange("p c r -> p (c r)").bitcast(I32))
         mask_rows = mask.rearrange("(p t) c -> t p c", t=PACK)
         out_rows = out_0.rearrange("(p t) c -> t p c", t=PACK)
-        for t in range(PACK):
-            nc.sync.dma_start(out=windows[t][:], in_=mask_rows[t])
 
         for q in range(QUADS):
             live = slice(32 * q, 32 * q + 4 * PASSES)
@@ -106,32 +106,52 @@ def tile_picked_zmae_mlpgelu_po_kernel(
                 in_=grouped[:, PACK * first : PACK * (first + count)],
             )
 
-        for g in range(PASSES):
-            grouped = keep.tile([P, H * PACK], BF16, name=f"w1_grouped{g}", align_bytes=64)
-            src = w1_raw[g][:].rearrange("p j (m t) -> p m j t", t=PACK)
-            dst = grouped[:].rearrange("p (t m j) -> p m j t", t=PACK, j=PACK)
-            split = W1_VECTOR_M[g]
-            nc.vector.tensor_copy(out=dst[:, :split], in_=src[:, :split])
-            nc.scalar.copy(out=dst[:, split:], in_=src[:, split:])
-            if g == 0:
-                gather_words(0, 0, S)
-                nc.vector.tensor_copy(
-                    out=w2_scale[:].rearrange("p (t m) -> p m t", t=PACK),
-                    in_=w2_scale_raw[:].rearrange("p (m t) -> p m t", t=PACK),
-                )
-                quantise_w1(0, grouped, 0, H)
-            else:
-                quantise_w1(1, grouped, 0, H // 2)
-                gather_words(1, 0, CHUNK)
-                quantise_w1(1, grouped, H // 2, H // 2)
-                gather_words(1, CHUNK, CHUNK)
-                gather_words(1, 2 * CHUNK, 2 * CHUNK)
+        w1_bf = [keep.tile([P, H * PACK], BF16, name=f"w1_bf{g}", tag=f"slot{3 + g}", align_bytes=64) for g in range(PASSES)]
+
+        def round_w1(u):
+            g, first, width, share = W1_PIECES[u]
+            src = w1_raw[u][:].rearrange("p j (m t) -> p m j t", t=PACK)
+            dst = w1_bf[g][:].rearrange("p (t m j) -> p m j t", t=PACK, j=PACK)[:, first // PACK : (first + width) // PACK]
+            split = share // PACK
+            if split > 0:
+                nc.vector.tensor_copy(out=dst[:, :split], in_=src[:, :split])
+            if share < width:
+                nc.scalar.copy(out=dst[:, split:], in_=src[:, split:])
+
+        gather_words(0, 0, S)
+        round_w1(0)
+        nc.vector.tensor_copy(
+            out=w2_scale[:].rearrange("p (t m) -> p m t", t=PACK),
+            in_=w2_scale_raw[:].rearrange("p (m t) -> p m t", t=PACK),
+        )
+        quantise_w1(0, w1_bf[0], 0, H)
+        warm_ps = psum.tile([P, S], F32, name="warm_ps", tag="bank7")
+        for t in range(WARM_PASSES):
+            m = slice(t * P, (t + 1) * P)
+            nc.tensor.matmul_mx(
+                out=warm_ps[:],
+                lhsT=w1_codes[0][:, m].bitcast(FP8X4),
+                lhsT_scale=w1_scale[0][:, m],
+                rhs=x_codes[0][:].bitcast(FP8X4),
+                rhs_scale=x_scale[:],
+                start=True,
+                stop=True,
+            )
+        round_w1(1)
+        round_w1(2)
+        quantise_w1(1, w1_bf[1], 0, H // 2)
+        gather_words(1, 0, CHUNK)
+        quantise_w1(1, w1_bf[1], H // 2, H // 2)
+        gather_words(1, CHUNK, CHUNK)
+        gather_words(1, 2 * CHUNK, 2 * CHUNK)
+
+        windows = [keep.tile([P, T], F32, name=f"window{t}", tag=f"slot{t}", align_bytes=64) for t in range(PACK)]
+        for t in range(PACK):
+            nc.sync.dma_start(out=windows[t][:], in_=mask_rows[t])
 
         h_bf = keep.tile([P, S * PACK], BF16, name="h_bf", align_bytes=64)
-        h_codes = keep.tile([P, S], U32, name="h_codes", align_bytes=64)
         h_scale = keep.tile([P, S], U8, name="h_scale", align_bytes=64)
         w2_codes = keep.tile([P, N], I32, name="w2_codes", align_bytes=64)
-        y_sb = [keep.tile([P, S], F32, name=f"y_sb{t}", align_bytes=64) for t in range(PACK)]
 
         def first_layer(c):
             cols = slice(c * CHUNK, (c + 1) * CHUNK)
@@ -154,34 +174,27 @@ def tile_picked_zmae_mlpgelu_po_kernel(
                 func=GELU,
             )
 
-        def quantise_h(first, count):
-            cols = slice(first, first + count)
+        def quantise_h(codes, first, count):
             nc.vector.quantize_mx(
-                out=h_codes[:, cols].bitcast(FP8X4),
-                scales=h_scale[:, cols],
+                out=codes.bitcast(FP8X4),
+                scales=h_scale[:, first : first + count],
                 in_=h_bf[:, PACK * first : PACK * (first + count)],
             )
 
-        def second_layer(t, first, count, bank):
-            cols = slice(first, first + count)
-            y_ps = psum.tile([P, count], F32, name=f"y_ps{t}_{first}", tag=f"bank{bank}")
+        def second_layer(y_ps, t, codes, first, count):
             m = slice(t * P, (t + 1) * P)
             nc.tensor.matmul_mx(
-                out=y_ps[:],
+                out=y_ps,
                 lhsT=w2_codes[:, m].bitcast(FP8X4),
                 lhsT_scale=w2_scale[:, m],
-                rhs=h_codes[:, cols].bitcast(FP8X4),
-                rhs_scale=h_scale[:, cols],
+                rhs=codes.bitcast(FP8X4),
+                rhs_scale=h_scale[:, first : first + count],
                 start=True,
                 stop=True,
             )
-            if t == 0 and first == 0:
-                nc.vector.tensor_copy(out=y_sb[t][:, cols], in_=y_ps[:])
-            else:
-                nc.scalar.copy(out=y_sb[t][:, cols], in_=y_ps[:])
 
-        def scatter(t, first, count):
-            nc.vector.tensor_copy(out=windows[t][:].indirect(picks(first, count)), in_=y_sb[t][:, first : first + count])
+        def scatter(t, first, count, y):
+            nc.vector.tensor_copy(out=windows[t][:].indirect(picks(first, count)), in_=y)
 
         for c in range(CHUNKS - 1):
             first_layer(c)
@@ -189,23 +202,39 @@ def tile_picked_zmae_mlpgelu_po_kernel(
             out=w2_codes[:].rearrange("p (t m) -> p m t", t=PACK),
             in_=w2_word_raw[:].rearrange("p (m t) -> p m t", t=PACK),
         )
-        quantise_h(0, CHUNK)
-        second_layer(0, 0, CHUNK, CHUNKS)
+        PAIR = 2 * CHUNK
+        h_codes_a = keep.tile([P, PAIR], U32, name="h_codes_a", align_bytes=64)
+        y_first = keep.tile([P, CHUNK], F32, name="y_first", tag="first_then_codes", align_bytes=64)
+        y_sb = [keep.tile([P, S], F32, name=f"y_sb{t}", align_bytes=64) for t in range(PACK)]
+
+        quantise_h(h_codes_a[:, :CHUNK], 0, CHUNK)
+        y_ps0 = psum.tile([P, CHUNK], F32, name="y_ps0", tag="bank4")
+        second_layer(y_ps0[:], 0, h_codes_a[:, :CHUNK], 0, CHUNK)
+        nc.vector.tensor_copy(out=y_first[:], in_=y_ps0[:])
         first_layer(CHUNKS - 1)
-        quantise_h(CHUNK, CHUNK)
-        second_layer(0, CHUNK, CHUNK, CHUNKS + 1)
-        scatter(0, 0, CHUNK)
-        quantise_h(2 * CHUNK, 2 * CHUNK)
-        second_layer(0, 2 * CHUNK, 2 * CHUNK, CHUNKS + 2)
-        scatter(0, CHUNK, CHUNK)
+        quantise_h(h_codes_a[:, CHUNK:], CHUNK, CHUNK)
+        y_ps1 = psum.tile([P, CHUNK], F32, name="y_ps1", tag="bank5")
+        second_layer(y_ps1[:], 0, h_codes_a[:, CHUNK:], CHUNK, CHUNK)
+        nc.scalar.copy(out=y_sb[0][:, CHUNK:PAIR], in_=y_ps1[:])
+        scatter(0, 0, CHUNK, y_first[:])
+
+        h_codes_b = keep.tile([P, PAIR], U32, name="h_codes_b", tag="first_then_codes", align_bytes=64)
+        quantise_h(h_codes_b[:], PAIR, PAIR)
+        y_ps2 = psum.tile([P, PAIR], F32, name="y_ps2", tag="bank6")
+        second_layer(y_ps2[:], 0, h_codes_b[:], PAIR, PAIR)
+        nc.scalar.copy(out=y_sb[0][:, PAIR:], in_=y_ps2[:])
+        scatter(0, CHUNK, CHUNK, y_sb[0][:, CHUNK:PAIR])
         for t in range(1, PACK):
-            second_layer(t, 0, S, t - 1)
-        scatter(0, 2 * CHUNK, 2 * CHUNK)
+            y_ps = psum.tile([P, S], F32, name=f"y_ps_t{t}", tag=f"bank{t - 1}")
+            second_layer(y_ps[:, :PAIR], t, h_codes_a[:], 0, PAIR)
+            second_layer(y_ps[:, PAIR:], t, h_codes_b[:], PAIR, PAIR)
+            nc.scalar.copy(out=y_sb[t][:], in_=y_ps[:])
+        scatter(0, PAIR, PAIR, y_sb[0][:, PAIR:])
 
         rounded = keep.tile([P, T, PACK], BF16, name="rounded", align_bytes=64)
         for t in range(PACK):
             if t > 0:
-                scatter(t, 0, S)
+                scatter(t, 0, S, y_sb[t][:])
             nc.sync.dma_start(out=out_rows[t], in_=windows[t][:])
             if t < PACK - 2:
                 nc.scalar.copy(out=rounded[:, :, t], in_=windows[t][:])

@@ -20,7 +20,7 @@ PASSES = K // (P * PACK)
 QUADS = 4
 CHUNK = 128
 CHUNKS = S // CHUNK
-W1_PIECES = ((0, 0, 512, 320), (1, 0, 256, 0), (1, 256, 256, 256))
+W1_PIECES = ((0, 0, 512, 320), (1, 0, 512, 352))
 WARM_PASSES = 2
 LAST_VECTOR_COLS = 640
 HALF = T // 2
@@ -75,7 +75,6 @@ def tile_picked_zmae_mlpgelu_po_kernel(
                 in_=w2_scales[0, 4 * q : 4 * q + 4, :].bitcast(I32),
             )
         load_w1(1)
-        load_w1(2)
         nc.sync.dma_start(out=x_word_table[1][:], in_=x_words[1].rearrange("p c r -> p (c r)").bitcast(I32))
         nc.sync.dma_start(out=w2_word_raw[:], in_=w2_words[0].rearrange("p c r -> p (c r)").bitcast(I32))
         mask_rows = mask.rearrange("(p t) c -> t p c", t=PACK)
@@ -106,7 +105,7 @@ def tile_picked_zmae_mlpgelu_po_kernel(
                 in_=grouped[:, PACK * first : PACK * (first + count)],
             )
 
-        w1_bf = [keep.tile([P, H * PACK], BF16, name=f"w1_bf{g}", tag=f"slot{3 + g}", align_bytes=64) for g in range(PASSES)]
+        w1_bf = [keep.tile([P, H * PACK], BF16, name=f"w1_bf{g}", tag=f"slot{2 + g}", align_bytes=64) for g in range(PASSES)]
 
         def round_w1(u):
             g, first, width, share = W1_PIECES[u]
@@ -138,7 +137,6 @@ def tile_picked_zmae_mlpgelu_po_kernel(
                 stop=True,
             )
         round_w1(1)
-        round_w1(2)
         quantise_w1(1, w1_bf[1], 0, H // 2)
         gather_words(1, 0, CHUNK)
         quantise_w1(1, w1_bf[1], H // 2, H // 2)

@@ -21,8 +21,9 @@ QUADS = 4
 CHUNK = 128
 CHUNKS = S // CHUNK
 W1_PIECES = ((0, 0, 512, 320), (1, 0, 512, 352))
-WARM_PASSES = 2
-LAST_VECTOR_COLS = 640
+WARM_PASSES = 3
+LAST_VECTOR_COLS = 512
+QUARTER = T // 4
 HALF = T // 2
 
 
@@ -117,6 +118,12 @@ def tile_picked_zmae_mlpgelu_po_kernel(
             if share < width:
                 nc.scalar.copy(out=dst[:, split:], in_=src[:, split:])
 
+        def round_w1_half(g, h, share):
+            src = w1_raw[g][:].rearrange("p j (m t) -> p m j t", t=PACK)[:, :, :, 2 * h : 2 * h + 2]
+            dst = w1_bf[g][:].rearrange("p (t m j) -> p m j t", t=PACK, j=PACK)[:, :, :, 2 * h : 2 * h + 2]
+            nc.vector.tensor_copy(out=dst[:, :share], in_=src[:, :share])
+            nc.scalar.copy(out=dst[:, share:], in_=src[:, share:])
+
         gather_words(0, 0, S)
         round_w1(0)
         nc.vector.tensor_copy(
@@ -136,7 +143,8 @@ def tile_picked_zmae_mlpgelu_po_kernel(
                 start=True,
                 stop=True,
             )
-        round_w1(1)
+        round_w1_half(1, 0, 84)
+        round_w1_half(1, 1, 48)
         quantise_w1(1, w1_bf[1], 0, H // 2)
         gather_words(1, 0, CHUNK)
         quantise_w1(1, w1_bf[1], H // 2, H // 2)
@@ -200,34 +208,31 @@ def tile_picked_zmae_mlpgelu_po_kernel(
             out=w2_codes[:].rearrange("p (t m) -> p m t", t=PACK),
             in_=w2_word_raw[:].rearrange("p (m t) -> p m t", t=PACK),
         )
-        PAIR = 2 * CHUNK
-        h_codes_a = keep.tile([P, PAIR], U32, name="h_codes_a", align_bytes=64)
-        y_first = keep.tile([P, CHUNK], F32, name="y_first", tag="first_then_codes", align_bytes=64)
+        h_codes = keep.tile([P, S], U32, name="h_codes", align_bytes=64)
         y_sb = [keep.tile([P, S], F32, name=f"y_sb{t}", align_bytes=64) for t in range(PACK)]
 
-        quantise_h(h_codes_a[:, :CHUNK], 0, CHUNK)
-        y_ps0 = psum.tile([P, CHUNK], F32, name="y_ps0", tag="bank4")
-        second_layer(y_ps0[:], 0, h_codes_a[:, :CHUNK], 0, CHUNK)
-        nc.vector.tensor_copy(out=y_first[:], in_=y_ps0[:])
-        first_layer(CHUNKS - 1)
-        quantise_h(h_codes_a[:, CHUNK:], CHUNK, CHUNK)
-        y_ps1 = psum.tile([P, CHUNK], F32, name="y_ps1", tag="bank5")
-        second_layer(y_ps1[:], 0, h_codes_a[:, CHUNK:], CHUNK, CHUNK)
-        nc.scalar.copy(out=y_sb[0][:, CHUNK:PAIR], in_=y_ps1[:])
-        scatter(0, 0, CHUNK, y_first[:])
+        def first_window(i, first, count):
+            cols = slice(first, first + count)
+            quantise_h(h_codes[:, cols], first, count)
+            y_ps = psum.tile([P, count], F32, name=f"y_ps{i}", tag=f"bank{4 + i}")
+            second_layer(y_ps[:], 0, h_codes[:, cols], first, count)
+            if i == 0:
+                nc.vector.tensor_copy(out=y_sb[0][:, cols], in_=y_ps[:])
+            else:
+                nc.scalar.copy(out=y_sb[0][:, cols], in_=y_ps[:])
+            scatter(0, first, count, y_sb[0][:, cols])
 
-        h_codes_b = keep.tile([P, PAIR], U32, name="h_codes_b", tag="first_then_codes", align_bytes=64)
-        quantise_h(h_codes_b[:], PAIR, PAIR)
-        y_ps2 = psum.tile([P, PAIR], F32, name="y_ps2", tag="bank6")
-        second_layer(y_ps2[:], 0, h_codes_b[:], PAIR, PAIR)
-        nc.scalar.copy(out=y_sb[0][:, PAIR:], in_=y_ps2[:])
-        scatter(0, CHUNK, CHUNK, y_sb[0][:, CHUNK:PAIR])
-        for t in range(1, PACK):
-            y_ps = psum.tile([P, S], F32, name=f"y_ps_t{t}", tag=f"bank{t - 1}")
-            second_layer(y_ps[:, :PAIR], t, h_codes_a[:], 0, PAIR)
-            second_layer(y_ps[:, PAIR:], t, h_codes_b[:], PAIR, PAIR)
-            nc.scalar.copy(out=y_sb[t][:], in_=y_ps[:])
-        scatter(0, PAIR, PAIR, y_sb[0][:, PAIR:])
+        def other_windows():
+            for t in range(1, PACK):
+                y_ps = psum.tile([P, S], F32, name=f"y_ps_t{t}", tag=f"bank{t - 1}")
+                second_layer(y_ps[:], t, h_codes[:], 0, S)
+                nc.scalar.copy(out=y_sb[t][:], in_=y_ps[:])
+
+        first_window(0, 0, CHUNK)
+        first_layer(CHUNKS - 1)
+        first_window(1, CHUNK, CHUNK)
+        first_window(2, 2 * CHUNK, 2 * CHUNK)
+        other_windows()
 
         rounded = keep.tile([P, T, PACK], BF16, name="rounded", align_bytes=64)
         for t in range(PACK):
@@ -243,21 +248,26 @@ def tile_picked_zmae_mlpgelu_po_kernel(
                 )
                 nc.scalar.copy(out=rounded[:, LAST_VECTOR_COLS:, t], in_=windows[t][:, LAST_VECTOR_COLS:])
         last = PACK - 1
-        nc.vector.tensor_copy(out=rounded[:, :HALF, last], in_=windows[last][:, :HALF])
-        nc.scalar.copy(out=rounded[:, LAST_VECTOR_COLS:, last], in_=windows[last][:, LAST_VECTOR_COLS:])
-        nc.vector.tensor_copy(out=rounded[:, HALF:LAST_VECTOR_COLS, last], in_=windows[last][:, HALF:LAST_VECTOR_COLS])
+        for i in range(4):
+            cols = slice(i * QUARTER, (i + 1) * QUARTER)
+            if i < 2:
+                nc.vector.tensor_copy(out=rounded[:, cols, last], in_=windows[last][:, cols])
+            else:
+                nc.scalar.copy(out=rounded[:, cols, last], in_=windows[last][:, cols])
 
         out_codes = keep.tile([P, T], I32, name="out_codes", align_bytes=64)
         out_scale = keep.tile([P, T], U8, name="out_scale", align_bytes=64)
         out_words = out_1[0].rearrange("p c r -> p (c r)").bitcast(I32)
-        for first, count in ((0, HALF), (HALF, HALF // 2), (HALF + HALF // 2, HALF // 2)):
-            cols = slice(first, first + count)
+        for i in range(4):
+            cols = slice(i * QUARTER, (i + 1) * QUARTER)
             nc.vector.quantize_mx(
                 out=out_codes[:, cols].bitcast(FP8X4),
                 scales=out_scale[:, cols],
                 in_=rounded[:, cols, :].rearrange("p c t -> p (c t)"),
             )
-            nc.sync.dma_start(out=out_words[:, cols], in_=out_codes[:, cols])
+            if i > 0:
+                stored = slice(0, HALF) if i == 1 else cols
+                nc.sync.dma_start(out=out_words[:, stored], in_=out_codes[:, stored])
         for q in range(QUADS):
             queue = nc.sync if q % 2 == 0 else nc.scalar
             queue.dma_start(

@@ -68,8 +68,8 @@ def tile_picked_zmae_mlpgelu_po_kernel(
                 in_=x_scales[:, 4 * q : 4 * q + 4, :].bitcast(I32),
             )
         nc.scalar.activation(out=warm_out[:], in_=warm_in[:], func=GELU)
-        nc.sync.dma_start(out=x_word_table[0][:], in_=x_words[0].rearrange("p c r -> p (c r)").bitcast(I32))
         load_w1(0)
+        nc.sync.dma_start(out=x_word_table[0][:], in_=x_words[0].rearrange("p c r -> p (c r)").bitcast(I32))
         for q in range(QUADS):
             nc.sync.dma_start(
                 out=w2_scale_raw[32 * q : 32 * q + 4, :].bitcast(I32),
@@ -124,13 +124,13 @@ def tile_picked_zmae_mlpgelu_po_kernel(
             nc.vector.tensor_copy(out=dst[:, :share], in_=src[:, :share])
             nc.scalar.copy(out=dst[:, share:], in_=src[:, share:])
 
-        gather_words(0, 0, S)
         round_w1(0)
+        quantise_w1(0, w1_bf[0], 0, H)
+        gather_words(0, 0, S)
         nc.vector.tensor_copy(
             out=w2_scale[:].rearrange("p (t m) -> p m t", t=PACK),
             in_=w2_scale_raw[:].rearrange("p (m t) -> p m t", t=PACK),
         )
-        quantise_w1(0, w1_bf[0], 0, H)
         warm_ps = psum.tile([P, S], F32, name="warm_ps", tag="bank7")
         for t in range(WARM_PASSES):
             m = slice(t * P, (t + 1) * P)
@@ -138,8 +138,8 @@ def tile_picked_zmae_mlpgelu_po_kernel(
                 out=warm_ps[:],
                 lhsT=w1_codes[0][:, m].bitcast(FP8X4),
                 lhsT_scale=w1_scale[0][:, m],
-                rhs=x_codes[0][:].bitcast(FP8X4),
-                rhs_scale=x_scale[:],
+                rhs=w1_codes[0][:].bitcast(FP8X4),
+                rhs_scale=w1_scale[0][:],
                 start=True,
                 stop=True,
             )

@@ -22,7 +22,7 @@ CHUNK = 128
 CHUNKS = S // CHUNK
 W1_PIECES = ((0, 0, 512, 320), (1, 0, 512, 352))
 WARM_PASSES = 3
-LAST_VECTOR_COLS = 512
+LAST_SCALAR_COLS = 384
 QUARTER = T // 4
 HALF = T // 2
 
@@ -211,63 +211,88 @@ def tile_picked_zmae_mlpgelu_po_kernel(
         h_codes = keep.tile([P, S], U32, name="h_codes", align_bytes=64)
         y_sb = [keep.tile([P, S], F32, name=f"y_sb{t}", align_bytes=64) for t in range(PACK)]
 
-        def first_window(i, first, count):
-            cols = slice(first, first + count)
-            quantise_h(h_codes[:, cols], first, count)
-            y_ps = psum.tile([P, count], F32, name=f"y_ps{i}", tag=f"bank{4 + i}")
-            second_layer(y_ps[:], 0, h_codes[:, cols], first, count)
-            if i == 0:
-                nc.vector.tensor_copy(out=y_sb[0][:, cols], in_=y_ps[:])
-            else:
-                nc.scalar.copy(out=y_sb[0][:, cols], in_=y_ps[:])
-            scatter(0, first, count, y_sb[0][:, cols])
-
-        def other_windows():
-            for t in range(1, PACK):
-                y_ps = psum.tile([P, S], F32, name=f"y_ps_t{t}", tag=f"bank{t - 1}")
-                second_layer(y_ps[:], t, h_codes[:], 0, S)
-                nc.scalar.copy(out=y_sb[t][:], in_=y_ps[:])
-
-        first_window(0, 0, CHUNK)
+        PAIR = 2 * CHUNK
+        chunk0, chunk1, pair1 = slice(0, CHUNK), slice(CHUNK, PAIR), slice(PAIR, S)
+        quantise_h(h_codes[:, chunk0], 0, CHUNK)
+        y_ps0 = psum.tile([P, CHUNK], F32, name="y_ps0", tag="bank4")
+        second_layer(y_ps0[:], 0, h_codes[:, chunk0], 0, CHUNK)
+        nc.vector.tensor_copy(out=y_sb[0][:, chunk0], in_=y_ps0[:])
+        scatter(0, 0, CHUNK, y_sb[0][:, chunk0])
         first_layer(CHUNKS - 1)
-        first_window(1, CHUNK, CHUNK)
-        first_window(2, 2 * CHUNK, 2 * CHUNK)
-        other_windows()
+        y_ps1 = psum.tile([P, PAIR], F32, name="y_ps1", tag="bank5")
+        y_early = keep.tile([P, PAIR], F32, name="y_early", align_bytes=64)
+        FILL = CHUNK // 2
+        zeros = keep.tile([P, FILL], F32, name="zeros", align_bytes=64)
+        nc.vector.memset(zeros[:], 0.0)
+        second_layer(y_ps1[:, CHUNK : CHUNK + FILL], 1, h_codes[:, :FILL], 0, FILL)
+        quantise_h(h_codes[:, chunk1], CHUNK, CHUNK)
+        second_layer(y_ps1[:, chunk0], 0, h_codes[:, chunk1], CHUNK, CHUNK)
+        nc.scalar.copy(out=y_early[:, : CHUNK + FILL], in_=y_ps1[:, : CHUNK + FILL])
+        quantise_h(h_codes[:, pair1], PAIR, PAIR)
+        scatter(0, CHUNK, CHUNK, y_early[:, chunk0])
+        nc.vector.tensor_tensor(windows[1][:].indirect(picks(0, FILL)), y_early[:, CHUNK : CHUNK + FILL], zeros[:], mybir.AluOpType.add)
+        y_ps2 = psum.tile([P, PAIR], F32, name="y_ps2", tag="bank6")
+        second_layer(y_ps2[:], 0, h_codes[:, pair1], PAIR, PAIR)
+        nc.scalar.copy(out=y_sb[0][:, pair1], in_=y_ps2[:])
+        scatter(0, PAIR, PAIR, y_sb[0][:, pair1])
+        y_ps3 = psum.tile([P, S], F32, name="y_ps3", tag="bank0")
+        second_layer(y_ps3[:, pair1], 1, h_codes[:, pair1], PAIR, PAIR)
+        second_layer(y_ps3[:, chunk1], 1, h_codes[:, chunk1], CHUNK, CHUNK)
+        second_layer(y_ps3[:, FILL:CHUNK], 1, h_codes[:, FILL:CHUNK], FILL, FILL)
+        nc.scalar.copy(out=y_sb[1][:, FILL:], in_=y_ps3[:, FILL:])
+        for t in range(2, PACK):
+            y_ps = psum.tile([P, S], F32, name=f"y_ps_t{t}", tag=f"bank{t - 1}")
+            second_layer(y_ps[:], t, h_codes[:], 0, S)
+            nc.scalar.copy(out=y_sb[t][:], in_=y_ps[:])
 
         rounded = keep.tile([P, T, PACK], BF16, name="rounded", align_bytes=64)
         for t in range(PACK):
-            if t > 0:
+            if t == 1:
+                scatter(t, FILL, S - FILL, y_sb[t][:, FILL:])
+            elif t > 1:
                 scatter(t, 0, S, y_sb[t][:])
             nc.sync.dma_start(out=out_rows[t], in_=windows[t][:])
             if t < PACK - 2:
                 nc.scalar.copy(out=rounded[:, :, t], in_=windows[t][:])
             elif t == PACK - 2:
                 nc.scalar.copy(
-                    out=rounded[:, :LAST_VECTOR_COLS, t:],
-                    in_=windows[t][:, :LAST_VECTOR_COLS].unsqueeze(2).to_broadcast([P, LAST_VECTOR_COLS, 2]),
+                    out=rounded[:, LAST_SCALAR_COLS:, t:],
+                    in_=windows[t][:, LAST_SCALAR_COLS:].unsqueeze(2).to_broadcast([P, T - LAST_SCALAR_COLS, 2]),
                 )
-                nc.scalar.copy(out=rounded[:, LAST_VECTOR_COLS:, t], in_=windows[t][:, LAST_VECTOR_COLS:])
+                nc.scalar.copy(out=rounded[:, :LAST_SCALAR_COLS, t], in_=windows[t][:, :LAST_SCALAR_COLS])
         last = PACK - 1
-        for i in range(4):
-            cols = slice(i * QUARTER, (i + 1) * QUARTER)
-            if i < 2:
-                nc.vector.tensor_copy(out=rounded[:, cols, last], in_=windows[last][:, cols])
-            else:
-                nc.scalar.copy(out=rounded[:, cols, last], in_=windows[last][:, cols])
-
         out_codes = keep.tile([P, T], I32, name="out_codes", align_bytes=64)
         out_scale = keep.tile([P, T], U8, name="out_scale", align_bytes=64)
         out_words = out_1[0].rearrange("p c r -> p (c r)").bitcast(I32)
-        for i in range(4):
-            cols = slice(i * QUARTER, (i + 1) * QUARTER)
+        quarter = [slice(i * QUARTER, (i + 1) * QUARTER) for i in range(4)]
+        EIGHTH = QUARTER // 2
+
+        def round_last(copy, cols):
+            copy(out=rounded[:, cols, last], in_=windows[last][:, cols])
+
+        def quantise_out(cols):
             nc.vector.quantize_mx(
                 out=out_codes[:, cols].bitcast(FP8X4),
                 scales=out_scale[:, cols],
                 in_=rounded[:, cols, :].rearrange("p c t -> p (c t)"),
             )
-            if i > 0:
-                stored = slice(0, HALF) if i == 1 else cols
-                nc.sync.dma_start(out=out_words[:, stored], in_=out_codes[:, stored])
+
+        def store_words(cols):
+            nc.sync.dma_start(out=out_words[:, cols], in_=out_codes[:, cols])
+
+        round_last(nc.scalar.copy, quarter[0])
+        round_last(nc.scalar.copy, slice(QUARTER, LAST_SCALAR_COLS))
+        round_last(nc.vector.tensor_copy, quarter[2])
+        round_last(nc.vector.tensor_copy, quarter[3])
+        quantise_out(quarter[2])
+        quantise_out(quarter[3])
+        store_words(slice(HALF, T))
+        round_last(nc.vector.tensor_copy, slice(LAST_SCALAR_COLS, HALF))
+        quantise_out(quarter[0])
+        quantise_out(slice(QUARTER, QUARTER + EIGHTH))
+        store_words(slice(0, QUARTER + EIGHTH))
+        quantise_out(slice(QUARTER + EIGHTH, HALF))
+        store_words(slice(QUARTER + EIGHTH, HALF))
         for q in range(QUADS):
             queue = nc.sync if q % 2 == 0 else nc.scalar
             queue.dma_start(

@@ -22,7 +22,8 @@ CHUNK = 128
 CHUNKS = S // CHUNK
 W1_PIECES = ((0, 0, 512, 320), (1, 0, 512, 352))
 WARM_PASSES = 3
-LAST_SCALAR_COLS = 384
+LAST_SCALAR_COLS = 512
+POOL_FIRST = 512
 QUARTER = T // 4
 HALF = T // 2
 
@@ -246,6 +247,10 @@ def tile_picked_zmae_mlpgelu_po_kernel(
             nc.scalar.copy(out=y_sb[t][:], in_=y_ps[:])
 
         rounded = keep.tile([P, T, PACK], BF16, name="rounded", align_bytes=64)
+
+        def pool_round(out, in_):
+            nc.gpsimd.tensor_scalar(out, in_, 1.0, -0.0, mybir.AluOpType.mult, mybir.AluOpType.add)
+
         for t in range(PACK):
             if t == 1:
                 scatter(t, FILL, S - FILL, y_sb[t][:, FILL:])
@@ -253,11 +258,12 @@ def tile_picked_zmae_mlpgelu_po_kernel(
                 scatter(t, 0, S, y_sb[t][:])
             nc.sync.dma_start(out=out_rows[t], in_=windows[t][:])
             if t < PACK - 2:
-                nc.scalar.copy(out=rounded[:, :, t], in_=windows[t][:])
+                nc.scalar.copy(out=rounded[:, :POOL_FIRST, t], in_=windows[t][:, :POOL_FIRST])
+                pool_round(rounded[:, POOL_FIRST:, t], windows[t][:, POOL_FIRST:])
             elif t == PACK - 2:
-                nc.scalar.copy(
-                    out=rounded[:, LAST_SCALAR_COLS:, t:],
-                    in_=windows[t][:, LAST_SCALAR_COLS:].unsqueeze(2).to_broadcast([P, T - LAST_SCALAR_COLS, 2]),
+                pool_round(
+                    rounded[:, POOL_FIRST:, t:],
+                    windows[t][:, POOL_FIRST:].unsqueeze(2).to_broadcast([P, T - POOL_FIRST, 2]),
                 )
                 nc.scalar.copy(out=rounded[:, :LAST_SCALAR_COLS, t], in_=windows[t][:, :LAST_SCALAR_COLS])
         last = PACK - 1
@@ -265,7 +271,6 @@ def tile_picked_zmae_mlpgelu_po_kernel(
         out_scale = keep.tile([P, T], U8, name="out_scale", align_bytes=64)
         out_words = out_1[0].rearrange("p c r -> p (c r)").bitcast(I32)
         quarter = [slice(i * QUARTER, (i + 1) * QUARTER) for i in range(4)]
-        EIGHTH = QUARTER // 2
 
         def round_last(copy, cols):
             copy(out=rounded[:, cols, last], in_=windows[last][:, cols])
@@ -281,18 +286,16 @@ def tile_picked_zmae_mlpgelu_po_kernel(
             nc.sync.dma_start(out=out_words[:, cols], in_=out_codes[:, cols])
 
         round_last(nc.scalar.copy, quarter[0])
-        round_last(nc.scalar.copy, slice(QUARTER, LAST_SCALAR_COLS))
+        round_last(nc.scalar.copy, quarter[1])
         round_last(nc.vector.tensor_copy, quarter[2])
         round_last(nc.vector.tensor_copy, quarter[3])
         quantise_out(quarter[2])
         quantise_out(quarter[3])
         store_words(slice(HALF, T))
-        round_last(nc.vector.tensor_copy, slice(LAST_SCALAR_COLS, HALF))
         quantise_out(quarter[0])
-        quantise_out(slice(QUARTER, QUARTER + EIGHTH))
-        store_words(slice(0, QUARTER + EIGHTH))
-        quantise_out(slice(QUARTER + EIGHTH, HALF))
-        store_words(slice(QUARTER + EIGHTH, HALF))
+        store_words(quarter[0])
+        quantise_out(quarter[1])
+        store_words(quarter[1])
         for q in range(QUADS):
             queue = nc.sync if q % 2 == 0 else nc.scalar
             queue.dma_start(

@@ -20,10 +20,10 @@ PASSES = K // (P * PACK)
 QUADS = 4
 CHUNK = 128
 CHUNKS = S // CHUNK
-W1_PIECES = ((0, 0, 512, 320), (1, 0, 512, 352))
+PAIR = 2 * CHUNK
+W1_FIRST_SHARE = 80
+W1_LAST_SHARES = (84, 48)
 WARM_PASSES = 3
-LAST_SCALAR_COLS = 512
-POOL_FIRST = 512
 QUARTER = T // 4
 HALF = T // 2
 
@@ -50,16 +50,16 @@ def tile_picked_zmae_mlpgelu_po_kernel(
         nc.vector.memset(warm_in[:], 0.0)
         nc.vector.memset(x_scale_table[:].bitcast(I32), 0)
 
-        w1_raw = [
-            keep.tile([P, PACK, width], F32, name=f"w1_raw{u}", tag=f"slot{u}", align_bytes=64) for u, (g, first, width, share) in enumerate(W1_PIECES)
-        ]
+        w1_raw = [keep.tile([P, PACK, H], F32, name=f"w1_raw{g}", tag=f"slot{g}", align_bytes=64) for g in range(PASSES)]
         x_word_table = [keep.tile([P, T], I32, name=f"x_word_table{g}", align_bytes=64) for g in range(PASSES)]
         w2_word_raw = keep.tile([P, N], I32, name="w2_word_raw", align_bytes=64)
 
-        def load_w1(u):
-            g, first, width, share = W1_PIECES[u]
-            rows = w1[g * 512 : (g + 1) * 512, first : first + width].rearrange("(p j) c -> p j c", j=PACK)
-            nc.sync.dma_start(out=w1_raw[u][:], in_=rows)
+        def load_w1(g):
+            rows = w1[g * 512 : (g + 1) * 512, :].rearrange("(p j) c -> p j c", j=PACK)
+            nc.sync.dma_start(out=w1_raw[g][:], in_=rows)
+
+        def load_x(g):
+            nc.sync.dma_start(out=x_word_table[g][:], in_=x_words[g].rearrange("p c r -> p (c r)").bitcast(I32))
 
         nc.sync.dma_start(offsets[:], offs)
         for q in range(QUADS):
@@ -70,14 +70,14 @@ def tile_picked_zmae_mlpgelu_po_kernel(
             )
         nc.scalar.activation(out=warm_out[:], in_=warm_in[:], func=GELU)
         load_w1(0)
-        nc.sync.dma_start(out=x_word_table[0][:], in_=x_words[0].rearrange("p c r -> p (c r)").bitcast(I32))
+        load_x(0)
         for q in range(QUADS):
             nc.sync.dma_start(
                 out=w2_scale_raw[32 * q : 32 * q + 4, :].bitcast(I32),
                 in_=w2_scales[0, 4 * q : 4 * q + 4, :].bitcast(I32),
             )
         load_w1(1)
-        nc.sync.dma_start(out=x_word_table[1][:], in_=x_words[1].rearrange("p c r -> p (c r)").bitcast(I32))
+        load_x(1)
         nc.sync.dma_start(out=w2_word_raw[:], in_=w2_words[0].rearrange("p c r -> p (c r)").bitcast(I32))
         mask_rows = mask.rearrange("(p t) c -> t p c", t=PACK)
         out_rows = out_0.rearrange("(p t) c -> t p c", t=PACK)
@@ -90,8 +90,25 @@ def tile_picked_zmae_mlpgelu_po_kernel(
 
         w1_codes = [keep.tile([P, H], U32, name=f"w1_codes{g}", align_bytes=64) for g in range(PASSES)]
         w1_scale = [keep.tile([P, H], U8, name=f"w1_scale{g}", align_bytes=64) for g in range(PASSES)]
-        x_codes = [keep.tile([P, S], U32, name=f"x_codes{g}", align_bytes=64) for g in range(PASSES)]
         w2_scale = keep.tile([P, N], U8, name="w2_scale", align_bytes=64)
+        w1_bf = [keep.tile([P, H * PACK], BF16, name=f"w1_bf{g}", tag=f"slot{2 + g}", align_bytes=64) for g in range(PASSES)]
+
+        def quantise_w1(g, first, count):
+            cols = slice(first, first + count)
+            nc.vector.quantize_mx(
+                out=w1_codes[g][:, cols].bitcast(FP8X4),
+                scales=w1_scale[g][:, cols],
+                in_=w1_bf[g][:, PACK * first : PACK * (first + count)],
+            )
+
+        def round_w1(g, tiles, share):
+            src = w1_raw[g][:].rearrange("p j (m t) -> p m j t", t=PACK)[:, :, :, tiles]
+            dst = w1_bf[g][:].rearrange("p (t m j) -> p m j t", t=PACK, j=PACK)[:, :, :, tiles]
+            nc.vector.tensor_copy(out=dst[:, :share], in_=src[:, :share])
+            nc.scalar.copy(out=dst[:, share:], in_=src[:, share:])
+
+        x_codes = [keep.tile([P, S], U32, name=f"x_codes{g}", align_bytes=64) for g in range(PASSES)]
+        h_ps = [psum.tile([P, PACK, CHUNK], F32, name=f"h_ps{c}", tag=f"bank{c}") for c in range(CHUNKS)]
 
         def gather_words(g, first, count):
             nc.vector.tensor_copy(
@@ -99,34 +116,22 @@ def tile_picked_zmae_mlpgelu_po_kernel(
                 in_=x_word_table[g][:].bitcast(U32).indirect(picks(first, count)),
             )
 
-        def quantise_w1(g, grouped, first, count):
-            cols = slice(first, first + count)
-            nc.vector.quantize_mx(
-                out=w1_codes[g][:, cols].bitcast(FP8X4),
-                scales=w1_scale[g][:, cols],
-                in_=grouped[:, PACK * first : PACK * (first + count)],
-            )
+        def first_layer(c, g):
+            cols = slice(c * CHUNK, (c + 1) * CHUNK)
+            for t in range(PACK):
+                m = slice(t * P, (t + 1) * P)
+                nc.tensor.matmul_mx(
+                    out=h_ps[c][:, t, :],
+                    lhsT=w1_codes[g][:, m].bitcast(FP8X4),
+                    lhsT_scale=w1_scale[g][:, m],
+                    rhs=x_codes[g][:, cols].bitcast(FP8X4),
+                    rhs_scale=x_scale[4 * g :, cols],
+                    start=(g == 0 and t == 0),
+                    stop=(g == PASSES - 1 and t == PACK - 1),
+                )
 
-        w1_bf = [keep.tile([P, H * PACK], BF16, name=f"w1_bf{g}", tag=f"slot{2 + g}", align_bytes=64) for g in range(PASSES)]
-
-        def round_w1(u):
-            g, first, width, share = W1_PIECES[u]
-            src = w1_raw[u][:].rearrange("p j (m t) -> p m j t", t=PACK)
-            dst = w1_bf[g][:].rearrange("p (t m j) -> p m j t", t=PACK, j=PACK)[:, first // PACK : (first + width) // PACK]
-            split = share // PACK
-            if split > 0:
-                nc.vector.tensor_copy(out=dst[:, :split], in_=src[:, :split])
-            if share < width:
-                nc.scalar.copy(out=dst[:, split:], in_=src[:, split:])
-
-        def round_w1_half(g, h, share):
-            src = w1_raw[g][:].rearrange("p j (m t) -> p m j t", t=PACK)[:, :, :, 2 * h : 2 * h + 2]
-            dst = w1_bf[g][:].rearrange("p (t m j) -> p m j t", t=PACK, j=PACK)[:, :, :, 2 * h : 2 * h + 2]
-            nc.vector.tensor_copy(out=dst[:, :share], in_=src[:, :share])
-            nc.scalar.copy(out=dst[:, share:], in_=src[:, share:])
-
-        round_w1(0)
-        quantise_w1(0, w1_bf[0], 0, H)
+        round_w1(0, slice(0, PACK), W1_FIRST_SHARE)
+        quantise_w1(0, 0, H)
         gather_words(0, 0, S)
         nc.vector.tensor_copy(
             out=w2_scale[:].rearrange("p (t m) -> p m t", t=PACK),
@@ -144,136 +149,118 @@ def tile_picked_zmae_mlpgelu_po_kernel(
                 start=True,
                 stop=True,
             )
-        round_w1_half(1, 0, 84)
-        round_w1_half(1, 1, 48)
-        quantise_w1(1, w1_bf[1], 0, H // 2)
+        for c in range(CHUNKS):
+            first_layer(c, 0)
+        round_w1(1, slice(0, 2), W1_LAST_SHARES[0])
+        round_w1(1, slice(2, 4), W1_LAST_SHARES[1])
+        quantise_w1(1, 0, H // 2)
         gather_words(1, 0, CHUNK)
-        quantise_w1(1, w1_bf[1], H // 2, H // 2)
+        quantise_w1(1, H // 2, H // 2)
         gather_words(1, CHUNK, CHUNK)
-        gather_words(1, 2 * CHUNK, 2 * CHUNK)
+        gather_words(1, PAIR, PAIR)
 
-        windows = [keep.tile([P, T], F32, name=f"window{t}", tag=f"slot{t}", align_bytes=64) for t in range(PACK)]
+        windows = [keep.tile([P, T], F32, name=f"window{t}", tag=f"slot{t}" if t > 1 else f"window{t}", align_bytes=64) for t in range(PACK)]
         for t in range(PACK):
             nc.sync.dma_start(out=windows[t][:], in_=mask_rows[t])
 
-        h_bf = keep.tile([P, S * PACK], BF16, name="h_bf", align_bytes=64)
         h_scale = keep.tile([P, S], U8, name="h_scale", align_bytes=64)
         w2_codes = keep.tile([P, N], I32, name="w2_codes", align_bytes=64)
 
-        def first_layer(c):
-            cols = slice(c * CHUNK, (c + 1) * CHUNK)
-            h_ps = psum.tile([P, PACK, CHUNK], F32, name=f"h_ps{c}", tag=f"bank{c}")
-            for t in range(PACK):
-                m = slice(t * P, (t + 1) * P)
-                for g in range(PASSES):
-                    nc.tensor.matmul_mx(
-                        out=h_ps[:, t, :],
-                        lhsT=w1_codes[g][:, m].bitcast(FP8X4),
-                        lhsT_scale=w1_scale[g][:, m],
-                        rhs=x_codes[g][:, cols].bitcast(FP8X4),
-                        rhs_scale=x_scale[4 * g :, cols],
-                        start=(g == 0),
-                        stop=(g == PASSES - 1),
-                    )
+        def gelu(c, out):
+            first_layer(c, 1)
             nc.scalar.activation(
-                out=h_bf[:, PACK * c * CHUNK : PACK * (c + 1) * CHUNK].rearrange("p (n t) -> p n t", t=PACK),
-                in_=h_ps[:].rearrange("p t n -> p n t"),
+                out=out.rearrange("p (n t) -> p n t", t=PACK),
+                in_=h_ps[c][:].rearrange("p t n -> p n t"),
                 func=GELU,
             )
 
-        def quantise_h(codes, first, count):
-            nc.vector.quantize_mx(
-                out=codes.bitcast(FP8X4),
-                scales=h_scale[:, first : first + count],
-                in_=h_bf[:, PACK * first : PACK * (first + count)],
-            )
+        def quantise_h(codes, first, values):
+            count = codes.shape[1]
+            nc.vector.quantize_mx(out=codes.bitcast(FP8X4), scales=h_scale[:, first : first + count], in_=values)
 
-        def second_layer(y_ps, t, codes, first, count):
+        def second_layer(y_ps, t, codes, first):
             m = slice(t * P, (t + 1) * P)
             nc.tensor.matmul_mx(
                 out=y_ps,
                 lhsT=w2_codes[:, m].bitcast(FP8X4),
                 lhsT_scale=w2_scale[:, m],
                 rhs=codes.bitcast(FP8X4),
-                rhs_scale=h_scale[:, first : first + count],
+                rhs_scale=h_scale[:, first : first + codes.shape[1]],
                 start=True,
                 stop=True,
             )
 
-        def scatter(t, first, count, y):
-            nc.vector.tensor_copy(out=windows[t][:].indirect(picks(first, count)), in_=y)
+        def scatter(t, first, y):
+            nc.vector.tensor_copy(out=windows[t][:].indirect(picks(first, y.shape[1])), in_=y)
 
-        for c in range(CHUNKS - 1):
-            first_layer(c)
+        h_early = keep.tile([P, 2, CHUNK * PACK], BF16, name="h_early", align_bytes=64)
+        gelu(0, h_early[:, 0, :])
         nc.vector.tensor_copy(
             out=w2_codes[:].rearrange("p (t m) -> p m t", t=PACK),
             in_=w2_word_raw[:].rearrange("p (m t) -> p m t", t=PACK),
         )
-        h_codes = keep.tile([P, S], U32, name="h_codes", align_bytes=64)
-        y_sb = [keep.tile([P, S], F32, name=f"y_sb{t}", align_bytes=64) for t in range(PACK)]
-
-        PAIR = 2 * CHUNK
-        chunk0, chunk1, pair1 = slice(0, CHUNK), slice(CHUNK, PAIR), slice(PAIR, S)
-        quantise_h(h_codes[:, chunk0], 0, CHUNK)
-        y_ps0 = psum.tile([P, CHUNK], F32, name="y_ps0", tag="bank4")
-        second_layer(y_ps0[:], 0, h_codes[:, chunk0], 0, CHUNK)
-        nc.vector.tensor_copy(out=y_sb[0][:, chunk0], in_=y_ps0[:])
-        scatter(0, 0, CHUNK, y_sb[0][:, chunk0])
-        first_layer(CHUNKS - 1)
-        y_ps1 = psum.tile([P, PAIR], F32, name="y_ps1", tag="bank5")
-        y_early = keep.tile([P, PAIR], F32, name="y_early", align_bytes=64)
-        FILL = CHUNK // 2
-        zeros = keep.tile([P, FILL], F32, name="zeros", align_bytes=64)
-        nc.vector.memset(zeros[:], 0.0)
-        second_layer(y_ps1[:, CHUNK : CHUNK + FILL], 1, h_codes[:, :FILL], 0, FILL)
-        quantise_h(h_codes[:, chunk1], CHUNK, CHUNK)
-        second_layer(y_ps1[:, chunk0], 0, h_codes[:, chunk1], CHUNK, CHUNK)
-        nc.scalar.copy(out=y_early[:, : CHUNK + FILL], in_=y_ps1[:, : CHUNK + FILL])
-        quantise_h(h_codes[:, pair1], PAIR, PAIR)
-        scatter(0, CHUNK, CHUNK, y_early[:, chunk0])
-        nc.vector.tensor_tensor(windows[1][:].indirect(picks(0, FILL)), y_early[:, CHUNK : CHUNK + FILL], zeros[:], mybir.AluOpType.add)
-        y_ps2 = psum.tile([P, PAIR], F32, name="y_ps2", tag="bank6")
-        second_layer(y_ps2[:], 0, h_codes[:, pair1], PAIR, PAIR)
-        nc.scalar.copy(out=y_sb[0][:, pair1], in_=y_ps2[:])
-        scatter(0, PAIR, PAIR, y_sb[0][:, pair1])
-        y_ps3 = psum.tile([P, S], F32, name="y_ps3", tag="bank0")
-        second_layer(y_ps3[:, pair1], 1, h_codes[:, pair1], PAIR, PAIR)
-        second_layer(y_ps3[:, chunk1], 1, h_codes[:, chunk1], CHUNK, CHUNK)
-        second_layer(y_ps3[:, FILL:CHUNK], 1, h_codes[:, FILL:CHUNK], FILL, FILL)
-        nc.scalar.copy(out=y_sb[1][:, FILL:], in_=y_ps3[:, FILL:])
+        codes0 = keep.tile([P, CHUNK], U32, name="codes0", tag="after_codes0", align_bytes=64)
+        quantise_h(codes0[:], 0, h_early[:, 0, :])
+        gelu(1, h_early[:, 1, :])
+        lead_ps = [psum.tile([P, CHUNK], F32, name=f"lead_ps{t}", tag=f"bank{4 + t}") for t in range(2)]
+        whole_ps = [psum.tile([P, S], F32, name=f"whole_ps{t}", tag=f"bank{4 + t}") for t in range(2, PACK)]
+        lead = [keep.tile([P, CHUNK], F32, name=f"lead{t}", align_bytes=64) for t in range(2)]
+        for t in range(2):
+            second_layer(lead_ps[t][:], t, codes0[:], 0)
+            nc.scalar.copy(out=lead[t][:], in_=lead_ps[t][:])
         for t in range(2, PACK):
-            y_ps = psum.tile([P, S], F32, name=f"y_ps_t{t}", tag=f"bank{t - 1}")
-            second_layer(y_ps[:], t, h_codes[:], 0, S)
-            nc.scalar.copy(out=y_sb[t][:], in_=y_ps[:])
+            second_layer(whole_ps[t - 2][:, :CHUNK], t, codes0[:], 0)
+        codes1 = keep.tile([P, CHUNK], U32, name="codes1", align_bytes=64)
+        quantise_h(codes1[:], CHUNK, h_early[:, 1, :])
+        for t in range(2):
+            scatter(t, 0, lead[t][:])
+        second_ps = psum.tile([P, 2, CHUNK], F32, name="second_ps", tag="bank0")
+        for t in range(2):
+            second_layer(second_ps[:, t, :], t, codes1[:], CHUNK)
+        for t in range(2, PACK):
+            second_layer(whole_ps[t - 2][:, CHUNK:PAIR], t, codes1[:], CHUNK)
+        h_late = keep.tile([P, 2, CHUNK * PACK], BF16, name="h_late", tag="after_codes0", align_bytes=64)
+        gelu(2, h_late[:, 0, :])
+        gelu(3, h_late[:, 1, :])
+        second = keep.tile([P, 2, CHUNK], F32, name="second", align_bytes=64)
+        nc.scalar.copy(out=second[:], in_=second_ps[:])
+        codes23 = keep.tile([P, PAIR], U32, name="codes23", align_bytes=64)
+        quantise_h(codes23[:], PAIR, h_late[:].rearrange("p c n -> p (c n)"))
+        for t in range(2):
+            scatter(t, CHUNK, second[:, t, :])
+        third_ps = psum.tile([P, 2, PAIR], F32, name="third_ps", tag="bank1")
+        for t in range(2):
+            second_layer(third_ps[:, t, :], t, codes23[:], PAIR)
+        third = keep.tile([P, 2, PAIR], F32, name="third", align_bytes=64)
+        nc.scalar.copy(out=third[:], in_=third_ps[:])
+        whole = [keep.tile([P, S], F32, name=f"whole{t}", align_bytes=64) for t in range(2, PACK)]
+        for t in range(2, PACK):
+            second_layer(whole_ps[t - 2][:, PAIR:], t, codes23[:], PAIR)
+            nc.scalar.copy(out=whole[t - 2][:], in_=whole_ps[t - 2][:])
 
         rounded = keep.tile([P, T, PACK], BF16, name="rounded", align_bytes=64)
+        quarter = [slice(i * QUARTER, (i + 1) * QUARTER) for i in range(4)]
+        low, high = slice(0, HALF), slice(HALF, T)
+        last = PACK - 1
 
         def pool_round(out, in_):
             nc.gpsimd.tensor_scalar(out, in_, 1.0, -0.0, mybir.AluOpType.mult, mybir.AluOpType.add)
 
         for t in range(PACK):
-            if t == 1:
-                scatter(t, FILL, S - FILL, y_sb[t][:, FILL:])
-            elif t > 1:
-                scatter(t, 0, S, y_sb[t][:])
+            if t < 2:
+                scatter(t, PAIR, third[:, t, :])
+            else:
+                scatter(t, 0, whole[t - 2][:])
             nc.sync.dma_start(out=out_rows[t], in_=windows[t][:])
-            if t < PACK - 2:
-                nc.scalar.copy(out=rounded[:, :POOL_FIRST, t], in_=windows[t][:, :POOL_FIRST])
-                pool_round(rounded[:, POOL_FIRST:, t], windows[t][:, POOL_FIRST:])
-            elif t == PACK - 2:
-                pool_round(
-                    rounded[:, POOL_FIRST:, t:],
-                    windows[t][:, POOL_FIRST:].unsqueeze(2).to_broadcast([P, T - POOL_FIRST, 2]),
-                )
-                nc.scalar.copy(out=rounded[:, :LAST_SCALAR_COLS, t], in_=windows[t][:, :LAST_SCALAR_COLS])
-        last = PACK - 1
+            if t < last - 1:
+                pool_round(rounded[:, low, t], windows[t][:, low])
+                nc.scalar.copy(out=rounded[:, high, t], in_=windows[t][:, high])
+            elif t < last:
+                pool_round(rounded[:, low, t:], windows[t][:, low].unsqueeze(2).to_broadcast([P, HALF, 2]))
+                nc.scalar.copy(out=rounded[:, high, t:], in_=windows[t][:, high].unsqueeze(2).to_broadcast([P, HALF, 2]))
         out_codes = keep.tile([P, T], I32, name="out_codes", align_bytes=64)
         out_scale = keep.tile([P, T], U8, name="out_scale", align_bytes=64)
         out_words = out_1[0].rearrange("p c r -> p (c r)").bitcast(I32)
-        quarter = [slice(i * QUARTER, (i + 1) * QUARTER) for i in range(4)]
-
-        def round_last(copy, cols):
-            copy(out=rounded[:, cols, last], in_=windows[last][:, cols])
 
         def quantise_out(cols):
             nc.vector.quantize_mx(
@@ -282,20 +269,16 @@ def tile_picked_zmae_mlpgelu_po_kernel(
                 in_=rounded[:, cols, :].rearrange("p c t -> p (c t)"),
             )
 
-        def store_words(cols):
-            nc.sync.dma_start(out=out_words[:, cols], in_=out_codes[:, cols])
-
-        round_last(nc.scalar.copy, quarter[0])
-        round_last(nc.scalar.copy, quarter[1])
-        round_last(nc.vector.tensor_copy, quarter[2])
-        round_last(nc.vector.tensor_copy, quarter[3])
-        quantise_out(quarter[2])
-        quantise_out(quarter[3])
-        store_words(slice(HALF, T))
-        quantise_out(quarter[0])
-        store_words(quarter[0])
-        quantise_out(quarter[1])
-        store_words(quarter[1])
+        for i in range(2):
+            nc.scalar.copy(out=rounded[:, quarter[i], last], in_=windows[last][:, quarter[i]])
+        for i in range(2, 4):
+            nc.vector.tensor_copy(out=rounded[:, quarter[i], last], in_=windows[last][:, quarter[i]])
+        for i in range(2, 4):
+            quantise_out(quarter[i])
+        nc.sync.dma_start(out=out_words[:, high], in_=out_codes[:, high])
+        for i in range(2):
+            quantise_out(quarter[i])
+            nc.sync.dma_start(out=out_words[:, quarter[i]], in_=out_codes[:, quarter[i]])
         for q in range(QUADS):
             queue = nc.sync if q % 2 == 0 else nc.scalar
             queue.dma_start(

@@ -21,9 +21,10 @@ QUADS = 4
 CHUNK = 128
 CHUNKS = S // CHUNK
 PAIR = 2 * CHUNK
-W1_FIRST_SHARE = 80
-W1_LAST_SHARES = (84, 48)
-WARM_PASSES = 3
+SHARE_PASS0 = 80
+SHARE_PASS1 = (84, 48)
+WARM_PASSES = 2
+EARLY, LATE = (2, 0), (1, 3)
 QUARTER = T // 4
 HALF = T // 2
 
@@ -36,27 +37,30 @@ def tile_picked_zmae_mlpgelu_po_kernel(
         keep = ctx.enter_context(tc.tile_pool(name="keep", bufs=1))
         psum = ctx.enter_context(tc.psum_pool(name="psum", bufs=1))
 
+        def tile(name, shape, dtype, tag=None):
+            return keep.tile(shape, dtype, name=name, tag=tag or name, align_bytes=64)
+
         offsets = keep.tile([P, S // 16], U16, name="offsets")
 
         def picks(first, count):
             return offsets[:, first // 16 : (first + count) // 16]
 
-        warm_in = keep.tile([P, 8], F32, name="warm_in")
-        warm_out = keep.tile([P, 8], F32, name="warm_out")
-        x_scale_table = keep.tile([P, T], U8, name="x_scale_table", align_bytes=64)
-        w2_scale_raw = keep.tile([P, N], U8, name="w2_scale_raw", align_bytes=64)
-        x_scale_rows = keep.tile([P, T], U8, name="x_scale_rows", align_bytes=64)
+        warm_in = tile("warm_in", [P, 8], F32)
+        warm_out = tile("warm_out", [P, 8], F32)
+        x_scale_rows = tile("x_scale_rows", [P, T], U8)
+        x_scale_table = tile("x_scale_table", [P, T], U8)
+        w2_scale_raw = tile("w2_scale_raw", [P, N], U8)
         nc.vector.memset(w2_scale_raw[:].bitcast(I32), 0)
-        nc.vector.memset(warm_in[:], 0.0)
+        nc.gpsimd.memset(warm_in[:], 0.0)
         nc.vector.memset(x_scale_table[:].bitcast(I32), 0)
 
-        w1_raw = [keep.tile([P, PACK, H], F32, name=f"w1_raw{g}", tag=f"slot{g}", align_bytes=64) for g in range(PASSES)]
-        x_word_table = [keep.tile([P, T], I32, name=f"x_word_table{g}", align_bytes=64) for g in range(PASSES)]
-        w2_word_raw = keep.tile([P, N], I32, name="w2_word_raw", align_bytes=64)
-
-        def load_w1(g):
-            rows = w1[g * 512 : (g + 1) * 512, :].rearrange("(p j) c -> p j c", j=PACK)
-            nc.sync.dma_start(out=w1_raw[g][:], in_=rows)
+        w1_rows = w1.rearrange("(g p j) c -> g p j c", g=PASSES, j=PACK)
+        w1_raw = [tile(f"w1_raw{g}", [P, PACK, H], F32) for g in range(PASSES)]
+        x_word_table = [tile(f"x_word_table{g}", [P, T], I32) for g in range(PASSES)]
+        w2_word_raw = tile("w2_word_raw", [P, N], I32)
+        windows = [tile(f"window{t}", [P, T], F32) for t in range(PACK)]
+        mask_rows = mask.rearrange("(p t) c -> t p c", t=PACK)
+        out_rows = out_0.rearrange("(p t) c -> t p c", t=PACK)
 
         def load_x(g):
             nc.sync.dma_start(out=x_word_table[g][:], in_=x_words[g].rearrange("p c r -> p (c r)").bitcast(I32))
@@ -69,29 +73,40 @@ def tile_picked_zmae_mlpgelu_po_kernel(
                 in_=x_scales[:, 4 * q : 4 * q + 4, :].bitcast(I32),
             )
         nc.scalar.activation(out=warm_out[:], in_=warm_in[:], func=GELU)
-        load_w1(0)
+        nc.sync.dma_start(out=w1_raw[0][:], in_=w1_rows[0])
         load_x(0)
         for q in range(QUADS):
             nc.sync.dma_start(
                 out=w2_scale_raw[32 * q : 32 * q + 4, :].bitcast(I32),
                 in_=w2_scales[0, 4 * q : 4 * q + 4, :].bitcast(I32),
             )
-        load_w1(1)
+        nc.sync.dma_start(out=w1_raw[1][:], in_=w1_rows[1])
         load_x(1)
         nc.sync.dma_start(out=w2_word_raw[:], in_=w2_words[0].rearrange("p c r -> p (c r)").bitcast(I32))
-        mask_rows = mask.rearrange("(p t) c -> t p c", t=PACK)
-        out_rows = out_0.rearrange("(p t) c -> t p c", t=PACK)
+        for t in EARLY + LATE:
+            nc.sync.dma_start(out=windows[t][:], in_=mask_rows[t])
 
         for q in range(QUADS):
             live = slice(32 * q, 32 * q + 4 * PASSES)
             nc.vector.tensor_copy(out=x_scale_table[live, :].bitcast(I32), in_=x_scale_rows[live, :].bitcast(I32))
-        x_scale = keep.tile([P, S], U8, name="x_scale", align_bytes=64)
+        x_scale = tile("x_scale", [P, S], U8)
         nc.vector.tensor_copy(out=x_scale[:], in_=x_scale_table[:].indirect(offsets[:]))
 
-        w1_codes = [keep.tile([P, H], U32, name=f"w1_codes{g}", align_bytes=64) for g in range(PASSES)]
-        w1_scale = [keep.tile([P, H], U8, name=f"w1_scale{g}", align_bytes=64) for g in range(PASSES)]
-        w2_scale = keep.tile([P, N], U8, name="w2_scale", align_bytes=64)
-        w1_bf = [keep.tile([P, H * PACK], BF16, name=f"w1_bf{g}", tag=f"slot{2 + g}", align_bytes=64) for g in range(PASSES)]
+        w1_bf = [tile(f"w1_bf{g}", [P, H * PACK], BF16) for g in range(PASSES)]
+        w1_codes = [tile(f"w1_codes{g}", [P, H], U32) for g in range(PASSES)]
+        w1_scale = [tile(f"w1_scale{g}", [P, H], U8) for g in range(PASSES)]
+        h_ps = [psum.tile([P, PACK, CHUNK], F32, name=f"h_ps{c}", tag=f"bank{c}") for c in range(CHUNKS)]
+
+        def round_w1(g, tiles, share):
+            src = w1_raw[g][:].rearrange("p j (m t) -> p m j t", t=PACK)[:, :, :, tiles]
+            dst = w1_bf[g][:].rearrange("p (t m j) -> p m j t", t=PACK, j=PACK)[:, :, :, tiles]
+            nc.vector.tensor_copy(out=dst[:, :share], in_=src[:, :share])
+            nc.scalar.copy(out=dst[:, share:], in_=src[:, share:])
+
+        def deal(dealt, raw):
+            nc.vector.tensor_copy(
+                out=dealt[:].rearrange("p (t m) -> p m t", t=PACK), in_=raw[:].rearrange("p (m t) -> p m t", t=PACK)
+            )
 
         def quantise_w1(g, first, count):
             cols = slice(first, first + count)
@@ -101,42 +116,28 @@ def tile_picked_zmae_mlpgelu_po_kernel(
                 in_=w1_bf[g][:, PACK * first : PACK * (first + count)],
             )
 
-        def round_w1(g, tiles, share):
-            src = w1_raw[g][:].rearrange("p j (m t) -> p m j t", t=PACK)[:, :, :, tiles]
-            dst = w1_bf[g][:].rearrange("p (t m j) -> p m j t", t=PACK, j=PACK)[:, :, :, tiles]
-            nc.vector.tensor_copy(out=dst[:, :share], in_=src[:, :share])
-            nc.scalar.copy(out=dst[:, share:], in_=src[:, share:])
+        def gather_words(codes, g, first):
+            nc.vector.tensor_copy(out=codes, in_=x_word_table[g][:].bitcast(U32).indirect(picks(first, codes.shape[1])))
 
-        x_codes = [keep.tile([P, S], U32, name=f"x_codes{g}", align_bytes=64) for g in range(PASSES)]
-        h_ps = [psum.tile([P, PACK, CHUNK], F32, name=f"h_ps{c}", tag=f"bank{c}") for c in range(CHUNKS)]
-
-        def gather_words(g, first, count):
-            nc.vector.tensor_copy(
-                out=x_codes[g][:, first : first + count],
-                in_=x_word_table[g][:].bitcast(U32).indirect(picks(first, count)),
-            )
-
-        def first_layer(c, g):
-            cols = slice(c * CHUNK, (c + 1) * CHUNK)
+        def first_layer(c, g, codes):
             for t in range(PACK):
                 m = slice(t * P, (t + 1) * P)
                 nc.tensor.matmul_mx(
                     out=h_ps[c][:, t, :],
                     lhsT=w1_codes[g][:, m].bitcast(FP8X4),
                     lhsT_scale=w1_scale[g][:, m],
-                    rhs=x_codes[g][:, cols].bitcast(FP8X4),
-                    rhs_scale=x_scale[4 * g :, cols],
+                    rhs=codes.bitcast(FP8X4),
+                    rhs_scale=x_scale[4 * g :, c * CHUNK : (c + 1) * CHUNK],
                     start=(g == 0 and t == 0),
                     stop=(g == PASSES - 1 and t == PACK - 1),
                 )
 
-        round_w1(0, slice(0, PACK), W1_FIRST_SHARE)
+        round_w1(0, slice(0, PACK), SHARE_PASS0)
         quantise_w1(0, 0, H)
-        gather_words(0, 0, S)
-        nc.vector.tensor_copy(
-            out=w2_scale[:].rearrange("p (t m) -> p m t", t=PACK),
-            in_=w2_scale_raw[:].rearrange("p (m t) -> p m t", t=PACK),
-        )
+        x_first = tile("x_first", [P, S], U32)
+        gather_words(x_first[:], 0, 0)
+        w2_scale = tile("w2_scale", [P, N], U8)
+        deal(w2_scale, w2_scale_raw)
         warm_ps = psum.tile([P, S], F32, name="warm_ps", tag="bank7")
         for t in range(WARM_PASSES):
             m = slice(t * P, (t + 1) * P)
@@ -150,24 +151,18 @@ def tile_picked_zmae_mlpgelu_po_kernel(
                 stop=True,
             )
         for c in range(CHUNKS):
-            first_layer(c, 0)
-        round_w1(1, slice(0, 2), W1_LAST_SHARES[0])
-        round_w1(1, slice(2, 4), W1_LAST_SHARES[1])
-        quantise_w1(1, 0, H // 2)
-        gather_words(1, 0, CHUNK)
-        quantise_w1(1, H // 2, H // 2)
-        gather_words(1, CHUNK, CHUNK)
-        gather_words(1, PAIR, PAIR)
+            first_layer(c, 0, x_first[:, c * CHUNK : (c + 1) * CHUNK])
+        for u in range(2):
+            round_w1(1, slice(2 * u, 2 * u + 2), SHARE_PASS1[u])
+        x_early = tile("x_early", [P, 2, CHUNK], U32)
+        for u in range(2):
+            quantise_w1(1, u * H // 2, H // 2)
+            gather_words(x_early[:, u, :], 1, u * CHUNK)
 
-        windows = [keep.tile([P, T], F32, name=f"window{t}", tag=f"slot{t}" if t > 1 else f"window{t}", align_bytes=64) for t in range(PACK)]
-        for t in range(PACK):
-            nc.sync.dma_start(out=windows[t][:], in_=mask_rows[t])
-
-        h_scale = keep.tile([P, S], U8, name="h_scale", align_bytes=64)
-        w2_codes = keep.tile([P, N], I32, name="w2_codes", align_bytes=64)
+        h_scale = tile("h_scale", [P, S], U8)
+        w2_codes = tile("w2_codes", [P, N], I32)
 
         def gelu(c, out):
-            first_layer(c, 1)
             nc.scalar.activation(
                 out=out.rearrange("p (n t) -> p n t", t=PACK),
                 in_=h_ps[c][:].rearrange("p t n -> p n t"),
@@ -193,73 +188,73 @@ def tile_picked_zmae_mlpgelu_po_kernel(
         def scatter(t, first, y):
             nc.vector.tensor_copy(out=windows[t][:].indirect(picks(first, y.shape[1])), in_=y)
 
-        h_early = keep.tile([P, 2, CHUNK * PACK], BF16, name="h_early", align_bytes=64)
-        gelu(0, h_early[:, 0, :])
-        nc.vector.tensor_copy(
-            out=w2_codes[:].rearrange("p (t m) -> p m t", t=PACK),
-            in_=w2_word_raw[:].rearrange("p (m t) -> p m t", t=PACK),
-        )
-        codes0 = keep.tile([P, CHUNK], U32, name="codes0", tag="after_codes0", align_bytes=64)
-        quantise_h(codes0[:], 0, h_early[:, 0, :])
-        gelu(1, h_early[:, 1, :])
-        lead_ps = [psum.tile([P, CHUNK], F32, name=f"lead_ps{t}", tag=f"bank{4 + t}") for t in range(2)]
-        whole_ps = [psum.tile([P, S], F32, name=f"whole_ps{t}", tag=f"bank{4 + t}") for t in range(2, PACK)]
-        lead = [keep.tile([P, CHUNK], F32, name=f"lead{t}", align_bytes=64) for t in range(2)]
-        for t in range(2):
-            second_layer(lead_ps[t][:], t, codes0[:], 0)
-            nc.scalar.copy(out=lead[t][:], in_=lead_ps[t][:])
-        for t in range(2, PACK):
-            second_layer(whole_ps[t - 2][:, :CHUNK], t, codes0[:], 0)
-        codes1 = keep.tile([P, CHUNK], U32, name="codes1", align_bytes=64)
-        quantise_h(codes1[:], CHUNK, h_early[:, 1, :])
-        for t in range(2):
-            scatter(t, 0, lead[t][:])
+        h_early = [tile(f"h_early{c}", [P, CHUNK * PACK], BF16) for c in range(2)]
+        for c in range(2):
+            first_layer(c, 1, x_early[:, c, :])
+            gelu(c, h_early[c][:])
+        x_late = tile("x_late", [P, PAIR], U32)
+        gather_words(x_late[:], 1, PAIR)
+        deal(w2_codes, w2_word_raw)
+        h_codes = tile("h_codes", [P, S], U32)
+        quantise_h(h_codes[:, :CHUNK], 0, h_early[0][:])
+        lead_ps = [psum.tile([P, CHUNK], F32, name=f"lead_ps{i}", tag=f"bank{4 + i}") for i in range(2)]
+        lead = [tile(f"lead{i}", [P, CHUNK], F32) for i in range(2)]
+        for i, t in enumerate(EARLY):
+            second_layer(lead_ps[i][:], t, h_codes[:, :CHUNK], 0)
+            nc.scalar.copy(out=lead[i][:], in_=lead_ps[i][:])
+        quantise_h(h_codes[:, CHUNK:PAIR], CHUNK, h_early[1][:])
+        for i, t in enumerate(EARLY):
+            scatter(t, 0, lead[i][:])
+        h_late = tile("h_late", [P, 2, CHUNK * PACK], BF16, tag="h_early1")
+        for c in range(2):
+            first_layer(2 + c, 1, x_late[:, c * CHUNK : (c + 1) * CHUNK])
+            gelu(2 + c, h_late[:, c, :])
         second_ps = psum.tile([P, 2, CHUNK], F32, name="second_ps", tag="bank0")
-        for t in range(2):
-            second_layer(second_ps[:, t, :], t, codes1[:], CHUNK)
-        for t in range(2, PACK):
-            second_layer(whole_ps[t - 2][:, CHUNK:PAIR], t, codes1[:], CHUNK)
-        h_late = keep.tile([P, 2, CHUNK * PACK], BF16, name="h_late", tag="after_codes0", align_bytes=64)
-        gelu(2, h_late[:, 0, :])
-        gelu(3, h_late[:, 1, :])
-        second = keep.tile([P, 2, CHUNK], F32, name="second", align_bytes=64)
+        for i, t in enumerate(EARLY):
+            second_layer(second_ps[:, i, :], t, h_codes[:, CHUNK:PAIR], CHUNK)
+        second = tile("second", [P, 2, CHUNK], F32)
         nc.scalar.copy(out=second[:], in_=second_ps[:])
-        codes23 = keep.tile([P, PAIR], U32, name="codes23", align_bytes=64)
-        quantise_h(codes23[:], PAIR, h_late[:].rearrange("p c n -> p (c n)"))
-        for t in range(2):
-            scatter(t, CHUNK, second[:, t, :])
+        quantise_h(h_codes[:, PAIR:], PAIR, h_late[:].rearrange("p c n -> p (c n)"))
+        for i, t in enumerate(EARLY):
+            scatter(t, CHUNK, second[:, i, :])
         third_ps = psum.tile([P, 2, PAIR], F32, name="third_ps", tag="bank1")
-        for t in range(2):
-            second_layer(third_ps[:, t, :], t, codes23[:], PAIR)
-        third = keep.tile([P, 2, PAIR], F32, name="third", align_bytes=64)
-        nc.scalar.copy(out=third[:], in_=third_ps[:])
-        whole = [keep.tile([P, S], F32, name=f"whole{t}", align_bytes=64) for t in range(2, PACK)]
-        for t in range(2, PACK):
-            second_layer(whole_ps[t - 2][:, PAIR:], t, codes23[:], PAIR)
-            nc.scalar.copy(out=whole[t - 2][:], in_=whole_ps[t - 2][:])
+        for i, t in enumerate(EARLY):
+            second_layer(third_ps[:, i, :], t, h_codes[:, PAIR:], PAIR)
+        third = tile("third", [P, 2, PAIR], F32)
+        for i in range(2):
+            nc.scalar.copy(out=third[:, i, :], in_=third_ps[:, i, :])
+        whole_ps = [psum.tile([P, S], F32, name=f"whole_ps{i}", tag=f"bank{6 + i}") for i in range(2)]
+        for i, t in enumerate(LATE):
+            second_layer(whole_ps[i][:], t, h_codes[:], 0)
+        whole = tile("whole", [P, S], F32)
+        nc.scalar.copy(out=whole[:], in_=whole_ps[0][:])
 
-        rounded = keep.tile([P, T, PACK], BF16, name="rounded", align_bytes=64)
+        rounded = tile("rounded", [P, T, PACK], BF16)
         quarter = [slice(i * QUARTER, (i + 1) * QUARTER) for i in range(4)]
         low, high = slice(0, HALF), slice(HALF, T)
-        last = PACK - 1
+        last = LATE[1]
 
         def pool_round(out, in_):
             nc.gpsimd.tensor_scalar(out, in_, 1.0, -0.0, mybir.AluOpType.mult, mybir.AluOpType.add)
 
-        for t in range(PACK):
-            if t < 2:
-                scatter(t, PAIR, third[:, t, :])
-            else:
-                scatter(t, 0, whole[t - 2][:])
+        def finish(t):
             nc.sync.dma_start(out=out_rows[t], in_=windows[t][:])
-            if t < last - 1:
-                pool_round(rounded[:, low, t], windows[t][:, low])
-                nc.scalar.copy(out=rounded[:, high, t], in_=windows[t][:, high])
-            elif t < last:
-                pool_round(rounded[:, low, t:], windows[t][:, low].unsqueeze(2).to_broadcast([P, HALF, 2]))
-                nc.scalar.copy(out=rounded[:, high, t:], in_=windows[t][:, high].unsqueeze(2).to_broadcast([P, HALF, 2]))
-        out_codes = keep.tile([P, T], I32, name="out_codes", align_bytes=64)
-        out_scale = keep.tile([P, T], U8, name="out_scale", align_bytes=64)
+            pool_round(rounded[:, low, t], windows[t][:, low])
+            nc.scalar.copy(out=rounded[:, high, t], in_=windows[t][:, high])
+
+        scatter(EARLY[0], PAIR, third[:, 0, :])
+        nc.sync.dma_start(out=out_rows[EARLY[0]], in_=windows[EARLY[0]][:])
+        nc.scalar.copy(out=rounded[:, :, EARLY[0]], in_=windows[EARLY[0]][:])
+        scatter(EARLY[1], PAIR, third[:, 1, :])
+        whole_last = tile("whole_last", [P, S], F32, tag="third")
+        nc.scalar.copy(out=whole_last[:], in_=whole_ps[1][:])
+        finish(EARLY[1])
+        scatter(LATE[0], 0, whole[:])
+        finish(LATE[0])
+        scatter(last, 0, whole_last[:])
+        nc.sync.dma_start(out=out_rows[last], in_=windows[last][:])
+        out_codes = tile("out_codes", [P, T], I32)
+        out_scale = tile("out_scale", [P, T], U8)
         out_words = out_1[0].rearrange("p c r -> p (c r)").bitcast(I32)
 
         def quantise_out(cols):
@@ -269,16 +264,19 @@ def tile_picked_zmae_mlpgelu_po_kernel(
                 in_=rounded[:, cols, :].rearrange("p c t -> p (c t)"),
             )
 
-        for i in range(2):
-            nc.scalar.copy(out=rounded[:, quarter[i], last], in_=windows[last][:, quarter[i]])
+        pieces = (quarter[0], slice(QUARTER, HALF - CHUNK), slice(HALF - CHUNK, HALF))
+        for cols in pieces:
+            nc.scalar.copy(out=rounded[:, cols, last], in_=windows[last][:, cols])
         for i in range(2, 4):
             nc.vector.tensor_copy(out=rounded[:, quarter[i], last], in_=windows[last][:, quarter[i]])
         for i in range(2, 4):
             quantise_out(quarter[i])
         nc.sync.dma_start(out=out_words[:, high], in_=out_codes[:, high])
-        for i in range(2):
-            quantise_out(quarter[i])
-            nc.sync.dma_start(out=out_words[:, quarter[i]], in_=out_codes[:, quarter[i]])
+        for cols in pieces[:2]:
+            quantise_out(cols)
+        nc.sync.dma_start(out=out_words[:, : HALF - CHUNK], in_=out_codes[:, : HALF - CHUNK])
+        quantise_out(pieces[2])
+        nc.sync.dma_start(out=out_words[:, pieces[2]], in_=out_codes[:, pieces[2]])
         for q in range(QUADS):
             queue = nc.sync if q % 2 == 0 else nc.scalar
             queue.dma_start(

@@ -51,7 +51,7 @@ def tile_picked_zmae_mlpgelu_po_kernel(
         x_scale_table = tile("x_scale_table", [P, T], U8)
         w2_scale_raw = tile("w2_scale_raw", [P, N], U8)
         nc.vector.memset(w2_scale_raw[:].bitcast(I32), 0)
-        nc.gpsimd.memset(warm_in[:], 0.0)
+        nc.vector.memset(warm_in[:], 0.0)
         nc.vector.memset(x_scale_table[:].bitcast(I32), 0)
 
         w1_rows = w1.rearrange("(g p j) c -> g p j c", g=PASSES, j=PACK)

@@ -13,6 +13,7 @@ U16 = mybir.dt.uint16
 U8 = mybir.dt.uint8
 FP8X4 = mybir.dt.float8_e4m3fn_x4
 GELU = mybir.ActivationFunctionType.Gelu_apprx_tanh
+COPY = mybir.ActivationFunctionType.Copy
 
 P = 128
 PACK = 4
@@ -24,9 +25,8 @@ PAIR = 2 * CHUNK
 SHARE_PASS0 = 80
 SHARE_PASS1 = (84, 48)
 WARM_PASSES = 2
-EARLY, LATE = (2, 0), (1, 3)
+A, B, C, D = range(PACK)
 QUARTER = T // 4
-HALF = T // 2
 
 
 def tile_picked_zmae_mlpgelu_po_kernel(
@@ -83,7 +83,7 @@ def tile_picked_zmae_mlpgelu_po_kernel(
         nc.sync.dma_start(out=w1_raw[1][:], in_=w1_rows[1])
         load_x(1)
         nc.sync.dma_start(out=w2_word_raw[:], in_=w2_words[0].rearrange("p c r -> p (c r)").bitcast(I32))
-        for t in EARLY + LATE:
+        for t in range(PACK):
             nc.sync.dma_start(out=windows[t][:], in_=mask_rows[t])
 
         for q in range(QUADS):
@@ -185,8 +185,16 @@ def tile_picked_zmae_mlpgelu_po_kernel(
                 stop=True,
             )
 
-        def scatter(t, first, y):
+        def vector_scatter(t, first, y):
             nc.vector.tensor_copy(out=windows[t][:].indirect(picks(first, y.shape[1])), in_=y)
+
+        def scalar_scatter(t, first, y):
+            nc.scalar.activation(out=windows[t][:].indirect(picks(first, y.shape[1])), in_=y, func=COPY)
+
+        def product(name, bank, t, first, count):
+            y_ps = psum.tile([P, count], F32, name=name + "_ps", tag=f"bank{bank}")
+            second_layer(y_ps[:], t, h_codes[:, first : first + count], first)
+            return y_ps, tile(name, [P, count], F32)
 
         h_early = [tile(f"h_early{c}", [P, CHUNK * PACK], BF16) for c in range(2)]
         for c in range(2):
@@ -197,62 +205,56 @@ def tile_picked_zmae_mlpgelu_po_kernel(
         deal(w2_codes, w2_word_raw)
         h_codes = tile("h_codes", [P, S], U32)
         quantise_h(h_codes[:, :CHUNK], 0, h_early[0][:])
-        lead_ps = [psum.tile([P, CHUNK], F32, name=f"lead_ps{i}", tag=f"bank{4 + i}") for i in range(2)]
-        lead = [tile(f"lead{i}", [P, CHUNK], F32) for i in range(2)]
-        for i, t in enumerate(EARLY):
-            second_layer(lead_ps[i][:], t, h_codes[:, :CHUNK], 0)
-            nc.scalar.copy(out=lead[i][:], in_=lead_ps[i][:])
+        a0_ps, a0 = product("a0", 4, A, 0, CHUNK)
+        nc.vector.tensor_copy(out=a0[:], in_=a0_ps[:])
         quantise_h(h_codes[:, CHUNK:PAIR], CHUNK, h_early[1][:])
-        for i, t in enumerate(EARLY):
-            scatter(t, 0, lead[i][:])
-        h_late = tile("h_late", [P, 2, CHUNK * PACK], BF16, tag="h_early1")
+        vector_scatter(A, 0, a0[:])
+        h_late = tile("h_late", [P, 2, CHUNK * PACK], BF16)
         for c in range(2):
             first_layer(2 + c, 1, x_late[:, c * CHUNK : (c + 1) * CHUNK])
             gelu(2 + c, h_late[:, c, :])
-        second_ps = psum.tile([P, 2, CHUNK], F32, name="second_ps", tag="bank0")
-        for i, t in enumerate(EARLY):
-            second_layer(second_ps[:, i, :], t, h_codes[:, CHUNK:PAIR], CHUNK)
-        second = tile("second", [P, 2, CHUNK], F32)
-        nc.scalar.copy(out=second[:], in_=second_ps[:])
+        a1_ps, a1 = product("a1", 5, A, CHUNK, CHUNK)
+        nc.scalar.copy(out=a1[:], in_=a1_ps[:])
+        b0_ps, b0 = product("b0", 6, B, 0, PAIR)
+        nc.scalar.copy(out=b0[:], in_=b0_ps[:])
         quantise_h(h_codes[:, PAIR:], PAIR, h_late[:].rearrange("p c n -> p (c n)"))
-        for i, t in enumerate(EARLY):
-            scatter(t, CHUNK, second[:, i, :])
-        third_ps = psum.tile([P, 2, PAIR], F32, name="third_ps", tag="bank1")
-        for i, t in enumerate(EARLY):
-            second_layer(third_ps[:, i, :], t, h_codes[:, PAIR:], PAIR)
-        third = tile("third", [P, 2, PAIR], F32)
-        for i in range(2):
-            nc.scalar.copy(out=third[:, i, :], in_=third_ps[:, i, :])
-        whole_ps = [psum.tile([P, S], F32, name=f"whole_ps{i}", tag=f"bank{6 + i}") for i in range(2)]
-        for i, t in enumerate(LATE):
-            second_layer(whole_ps[i][:], t, h_codes[:], 0)
-        whole = tile("whole", [P, S], F32)
-        nc.scalar.copy(out=whole[:], in_=whole_ps[0][:])
+        vector_scatter(A, CHUNK, a1[:])
+        scalar_scatter(B, 0, b0[:])
+        a2_ps, a2 = product("a2", 0, A, PAIR, PAIR)
+        nc.vector.tensor_copy(out=a2[:], in_=a2_ps[:])
+        c_ps, c_all = product("c_all", 1, C, 0, S)
+        nc.vector.tensor_copy(out=c_all[:], in_=c_ps[:])
+        b1_ps, b1 = product("b1", 2, B, PAIR, PAIR)
+        nc.scalar.copy(out=b1[:], in_=b1_ps[:])
+        d_ps, d_all = product("d_all", 3, D, 0, S)
+        nc.scalar.copy(out=d_all[:], in_=d_ps[:])
 
+        pairs = tile("pairs", [P, 2, T, 2], BF16)
         rounded = tile("rounded", [P, T, PACK], BF16)
+        pair_words = pairs[:].rearrange("p u c e -> p u (c e)").bitcast(U32)
+        rounded_words = rounded[:].rearrange("p c t -> p (c t)").bitcast(U32).rearrange("p (c u) -> p c u", u=2)
         quarter = [slice(i * QUARTER, (i + 1) * QUARTER) for i in range(4)]
-        low, high = slice(0, HALF), slice(HALF, T)
-        last = LATE[1]
 
-        def pool_round(out, in_):
-            nc.gpsimd.tensor_scalar(out, in_, 1.0, -0.0, mybir.AluOpType.mult, mybir.AluOpType.add)
-
-        def finish(t):
+        def store(t):
             nc.sync.dma_start(out=out_rows[t], in_=windows[t][:])
-            pool_round(rounded[:, low, t], windows[t][:, low])
-            nc.scalar.copy(out=rounded[:, high, t], in_=windows[t][:, high])
 
-        scatter(EARLY[0], PAIR, third[:, 0, :])
-        nc.sync.dma_start(out=out_rows[EARLY[0]], in_=windows[EARLY[0]][:])
-        nc.scalar.copy(out=rounded[:, :, EARLY[0]], in_=windows[EARLY[0]][:])
-        scatter(EARLY[1], PAIR, third[:, 1, :])
-        whole_last = tile("whole_last", [P, S], F32, tag="third")
-        nc.scalar.copy(out=whole_last[:], in_=whole_ps[1][:])
-        finish(EARLY[1])
-        scatter(LATE[0], 0, whole[:])
-        finish(LATE[0])
-        scatter(last, 0, whole_last[:])
-        nc.sync.dma_start(out=out_rows[last], in_=windows[last][:])
+        def pool_round(t):
+            nc.gpsimd.tensor_scalar(
+                pairs[:, t // 2, :, t % 2], windows[t][:], 1.0, -0.0, mybir.AluOpType.mult, mybir.AluOpType.add
+            )
+
+        vector_scatter(A, PAIR, a2[:])
+        store(A)
+        pool_round(A)
+        scalar_scatter(B, PAIR, b1[:])
+        store(B)
+        pool_round(B)
+        vector_scatter(C, 0, c_all[:])
+        store(C)
+        nc.vector.tensor_copy(out=pairs[:, 1, :, 0], in_=windows[C][:])
+        for first in (0, PAIR):
+            scalar_scatter(D, first, d_all[:, first : first + PAIR])
+        store(D)
         out_codes = tile("out_codes", [P, T], I32)
         out_scale = tile("out_scale", [P, T], U8)
         out_words = out_1[0].rearrange("p c r -> p (c r)").bitcast(I32)
@@ -264,19 +266,19 @@ def tile_picked_zmae_mlpgelu_po_kernel(
                 in_=rounded[:, cols, :].rearrange("p c t -> p (c t)"),
             )
 
-        pieces = (quarter[0], slice(QUARTER, HALF - CHUNK), slice(HALF - CHUNK, HALF))
-        for cols in pieces:
-            nc.scalar.copy(out=rounded[:, cols, last], in_=windows[last][:, cols])
-        for i in range(2, 4):
-            nc.vector.tensor_copy(out=rounded[:, quarter[i], last], in_=windows[last][:, quarter[i]])
-        for i in range(2, 4):
+        for cols in quarter:
+            nc.vector.tensor_copy(out=pairs[:, 1, cols, 1], in_=windows[D][:, cols])
+        for cols in quarter[:3]:
+            nc.scalar.copy(out=rounded_words[:, cols, :], in_=pair_words[:, :, cols].rearrange("p u c -> p c u"))
+        nc.vector.tensor_copy(
+            out=rounded_words[:, quarter[3], :].bitcast(I32),
+            in_=pair_words[:, :, quarter[3]].bitcast(I32).rearrange("p u c -> p c u"),
+        )
+        for i in (0, 3, 1, 2):
             quantise_out(quarter[i])
-        nc.sync.dma_start(out=out_words[:, high], in_=out_codes[:, high])
-        for cols in pieces[:2]:
-            quantise_out(cols)
-        nc.sync.dma_start(out=out_words[:, : HALF - CHUNK], in_=out_codes[:, : HALF - CHUNK])
-        quantise_out(pieces[2])
-        nc.sync.dma_start(out=out_words[:, pieces[2]], in_=out_codes[:, pieces[2]])
+            if i != 0:
+                cols = slice(0, 2 * QUARTER) if i == 1 else quarter[i]
+                nc.sync.dma_start(out=out_words[:, cols], in_=out_codes[:, cols])
         for q in range(QUADS):
             queue = nc.sync if q % 2 == 0 else nc.scalar
             queue.dma_start(

@@ -75,14 +75,14 @@ def tile_picked_zmae_mlpgelu_po_kernel(
         nc.scalar.activation(out=warm_out[:], in_=warm_in[:], func=GELU)
         nc.sync.dma_start(out=w1_raw[0][:], in_=w1_rows[0])
         load_x(0)
+        nc.sync.dma_start(out=w1_raw[1][:], in_=w1_rows[1])
+        load_x(1)
+        nc.sync.dma_start(out=w2_word_raw[:], in_=w2_words[0].rearrange("p c r -> p (c r)").bitcast(I32))
         for q in range(QUADS):
             nc.sync.dma_start(
                 out=w2_scale_raw[32 * q : 32 * q + 4, :].bitcast(I32),
                 in_=w2_scales[0, 4 * q : 4 * q + 4, :].bitcast(I32),
             )
-        nc.sync.dma_start(out=w1_raw[1][:], in_=w1_rows[1])
-        load_x(1)
-        nc.sync.dma_start(out=w2_word_raw[:], in_=w2_words[0].rearrange("p c r -> p (c r)").bitcast(I32))
         for t in range(PACK):
             nc.sync.dma_start(out=windows[t][:], in_=mask_rows[t])
 
@@ -103,10 +103,8 @@ def tile_picked_zmae_mlpgelu_po_kernel(
             nc.vector.tensor_copy(out=dst[:, :share], in_=src[:, :share])
             nc.scalar.copy(out=dst[:, share:], in_=src[:, share:])
 
-        def deal(dealt, raw):
-            nc.vector.tensor_copy(
-                out=dealt[:].rearrange("p (t m) -> p m t", t=PACK), in_=raw[:].rearrange("p (m t) -> p m t", t=PACK)
-            )
+        def deal(copy, dealt, raw):
+            copy(out=dealt.rearrange("p (t m) -> p m t", t=PACK), in_=raw.rearrange("p (m t) -> p m t", t=PACK))
 
         def quantise_w1(g, first, count):
             cols = slice(first, first + count)
@@ -136,8 +134,6 @@ def tile_picked_zmae_mlpgelu_po_kernel(
         quantise_w1(0, 0, H)
         x_first = tile("x_first", [P, S], U32)
         gather_words(x_first[:], 0, 0)
-        w2_scale = tile("w2_scale", [P, N], U8)
-        deal(w2_scale, w2_scale_raw)
         warm_ps = psum.tile([P, S], F32, name="warm_ps", tag="bank7")
         for t in range(WARM_PASSES):
             m = slice(t * P, (t + 1) * P)
@@ -162,15 +158,16 @@ def tile_picked_zmae_mlpgelu_po_kernel(
         h_scale = tile("h_scale", [P, S], U8)
         w2_codes = tile("w2_codes", [P, N], I32)
 
-        def gelu(c, out):
+        def gelu(c):
             nc.scalar.activation(
-                out=out.rearrange("p (n t) -> p n t", t=PACK),
+                out=h_bf[:, c * CHUNK * PACK : (c + 1) * CHUNK * PACK].rearrange("p (n t) -> p n t", t=PACK),
                 in_=h_ps[c][:].rearrange("p t n -> p n t"),
                 func=GELU,
             )
 
-        def quantise_h(codes, first, values):
+        def quantise_h(codes, first):
             count = codes.shape[1]
+            values = h_bf[:, first * PACK : (first + count) * PACK]
             nc.vector.quantize_mx(out=codes.bitcast(FP8X4), scales=h_scale[:, first : first + count], in_=values)
 
         def second_layer(y_ps, t, codes, first):
@@ -191,47 +188,48 @@ def tile_picked_zmae_mlpgelu_po_kernel(
         def scalar_scatter(t, first, y):
             nc.scalar.activation(out=windows[t][:].indirect(picks(first, y.shape[1])), in_=y, func=COPY)
 
-        def product(name, bank, t, first, count):
-            y_ps = psum.tile([P, count], F32, name=name + "_ps", tag=f"bank{bank}")
-            second_layer(y_ps[:], t, h_codes[:, first : first + count], first)
-            return y_ps, tile(name, [P, count], F32)
+        def product(copy, bank, t, first, y):
+            count = y.shape[1]
+            y_ps = psum.tile([P, count], F32, name=f"y_ps{t}_{first}", tag=f"bank{bank}")
+            codes = h_codes[:, first : first + count] if first < PAIR else late_codes[:]
+            second_layer(y_ps[:], t, codes, first)
+            copy(out=y, in_=y_ps[:])
 
-        h_early = [tile(f"h_early{c}", [P, CHUNK * PACK], BF16) for c in range(2)]
+        deal(nc.scalar.copy, w2_codes[:].bitcast(U32), w2_word_raw[:].bitcast(U32))
+        h_bf = tile("h_bf", [P, S * PACK], BF16, tag="w2_word_raw")
         for c in range(2):
             first_layer(c, 1, x_early[:, c, :])
-            gelu(c, h_early[c][:])
+            gelu(c)
         x_late = tile("x_late", [P, PAIR], U32)
         gather_words(x_late[:], 1, PAIR)
-        deal(w2_codes, w2_word_raw)
-        h_codes = tile("h_codes", [P, S], U32)
-        quantise_h(h_codes[:, :CHUNK], 0, h_early[0][:])
-        a0_ps, a0 = product("a0", 4, A, 0, CHUNK)
-        nc.vector.tensor_copy(out=a0[:], in_=a0_ps[:])
-        quantise_h(h_codes[:, CHUNK:PAIR], CHUNK, h_early[1][:])
+        w2_scale = tile("w2_scale", [P, N], U8)
+        deal(nc.vector.tensor_copy, w2_scale[:], w2_scale_raw[:])
+        h_codes = tile("h_codes", [P, PAIR], U32, tag="w2_scale_raw")
+        quantise_h(h_codes[:, :CHUNK], 0)
+        a0, a1 = (tile(f"a{i}", [P, CHUNK], F32) for i in range(2))
+        a2, b0, b1, d0, d1 = (tile(name, [P, PAIR], F32) for name in ("a2", "b0", "b1", "d0", "d1"))
+        c_all = tile("c_all", [P, S], F32)
+        product(nc.vector.tensor_copy, 4, A, 0, a0[:])
+        quantise_h(h_codes[:, CHUNK:PAIR], CHUNK)
         vector_scatter(A, 0, a0[:])
-        h_late = tile("h_late", [P, 2, CHUNK * PACK], BF16)
         for c in range(2):
             first_layer(2 + c, 1, x_late[:, c * CHUNK : (c + 1) * CHUNK])
-            gelu(2 + c, h_late[:, c, :])
-        a1_ps, a1 = product("a1", 5, A, CHUNK, CHUNK)
-        nc.scalar.copy(out=a1[:], in_=a1_ps[:])
-        b0_ps, b0 = product("b0", 6, B, 0, PAIR)
-        nc.scalar.copy(out=b0[:], in_=b0_ps[:])
-        quantise_h(h_codes[:, PAIR:], PAIR, h_late[:].rearrange("p c n -> p (c n)"))
+            gelu(2 + c)
+        product(nc.scalar.copy, 5, A, CHUNK, a1[:])
+        product(nc.scalar.copy, 6, B, 0, b0[:])
+        product(nc.scalar.copy, 7, D, 0, d0[:])
+        product(nc.vector.tensor_copy, 0, C, 0, c_all[:, :PAIR])
+        late_codes = tile("late_codes", [P, PAIR], U32, tag="a0")
+        quantise_h(late_codes[:], PAIR)
         vector_scatter(A, CHUNK, a1[:])
         scalar_scatter(B, 0, b0[:])
-        a2_ps, a2 = product("a2", 0, A, PAIR, PAIR)
-        nc.vector.tensor_copy(out=a2[:], in_=a2_ps[:])
-        c_ps, c_all = product("c_all", 1, C, 0, S)
-        nc.vector.tensor_copy(out=c_all[:], in_=c_ps[:])
-        b1_ps, b1 = product("b1", 2, B, PAIR, PAIR)
-        nc.scalar.copy(out=b1[:], in_=b1_ps[:])
-        d_ps, d_all = product("d_all", 3, D, 0, S)
-        nc.scalar.copy(out=d_all[:], in_=d_ps[:])
+        product(nc.vector.tensor_copy, 1, A, PAIR, a2[:])
+        product(nc.vector.tensor_copy, 4, C, PAIR, c_all[:, PAIR:])
+        product(nc.scalar.copy, 2, B, PAIR, b1[:])
+        product(nc.scalar.copy, 3, D, PAIR, d1[:])
 
-        pairs = tile("pairs", [P, 2, T, 2], BF16)
+        pairs = tile("pairs", [P, 2, T - QUARTER, 2], BF16)
         rounded = tile("rounded", [P, T, PACK], BF16)
-        pair_words = pairs[:].rearrange("p u c e -> p u (c e)").bitcast(U32)
         rounded_words = rounded[:].rearrange("p c t -> p (c t)").bitcast(U32).rearrange("p (c u) -> p c u", u=2)
         quarter = [slice(i * QUARTER, (i + 1) * QUARTER) for i in range(4)]
 
@@ -240,7 +238,7 @@ def tile_picked_zmae_mlpgelu_po_kernel(
 
         def pool_round(t):
             nc.gpsimd.tensor_scalar(
-                pairs[:, t // 2, :, t % 2], windows[t][:], 1.0, -0.0, mybir.AluOpType.mult, mybir.AluOpType.add
+                pairs[:, t // 2, :, t % 2], windows[t][:, QUARTER:], 1.0, -0.0, mybir.AluOpType.mult, mybir.AluOpType.add
             )
 
         vector_scatter(A, PAIR, a2[:])
@@ -251,10 +249,20 @@ def tile_picked_zmae_mlpgelu_po_kernel(
         pool_round(B)
         vector_scatter(C, 0, c_all[:])
         store(C)
-        nc.vector.tensor_copy(out=pairs[:, 1, :, 0], in_=windows[C][:])
-        for first in (0, PAIR):
-            scalar_scatter(D, first, d_all[:, first : first + PAIR])
+        nc.vector.tensor_copy(out=pairs[:, 1, :, 0], in_=windows[C][:, QUARTER:])
+        scalar_scatter(D, 0, d0[:])
+        scalar_scatter(D, PAIR, d1[:])
         store(D)
+        first_pairs = tile("first_pairs", [P, 2, QUARTER, 2], BF16, tag="d0")
+        for t in (A, B):
+            nc.scalar.copy(out=first_pairs[:, 0, :, t], in_=windows[t][:, :QUARTER])
+        nc.vector.tensor_copy(out=first_pairs[:, 1, :, 0], in_=windows[C][:, :QUARTER])
+
+        def pairs_of(cols):
+            if cols.start < QUARTER:
+                return first_pairs[:, :, cols, :]
+            return pairs[:, :, cols.start - QUARTER : cols.stop - QUARTER, :]
+
         out_codes = tile("out_codes", [P, T], I32)
         out_scale = tile("out_scale", [P, T], U8)
         out_words = out_1[0].rearrange("p c r -> p (c r)").bitcast(I32)
@@ -266,19 +274,27 @@ def tile_picked_zmae_mlpgelu_po_kernel(
                 in_=rounded[:, cols, :].rearrange("p c t -> p (c t)"),
             )
 
-        for cols in quarter:
-            nc.vector.tensor_copy(out=pairs[:, 1, cols, 1], in_=windows[D][:, cols])
-        for cols in quarter[:3]:
-            nc.scalar.copy(out=rounded_words[:, cols, :], in_=pair_words[:, :, cols].rearrange("p u c -> p c u"))
-        nc.vector.tensor_copy(
-            out=rounded_words[:, quarter[3], :].bitcast(I32),
-            in_=pair_words[:, :, quarter[3]].bitcast(I32).rearrange("p u c -> p c u"),
-        )
-        for i in (0, 3, 1, 2):
-            quantise_out(quarter[i])
-            if i != 0:
-                cols = slice(0, 2 * QUARTER) if i == 1 else quarter[i]
-                nc.sync.dma_start(out=out_words[:, cols], in_=out_codes[:, cols])
+        def weave(copy, dtype, cols):
+            copy(out=rounded_words[:, cols, :].bitcast(dtype), in_=pairs_of(cols).rearrange("p u c e -> p u (c e)").bitcast(dtype).rearrange("p u c -> p c u"))
+
+        def store_words(cols):
+            nc.sync.dma_start(out=out_words[:, cols], in_=out_codes[:, cols])
+
+        border = 2 * QUARTER + CHUNK
+        first_cols, vector_cols = quarter[0], slice(QUARTER, border)
+        late_cols, last_cols = slice(border, T - CHUNK), slice(T - CHUNK, T)
+        for cols in (first_cols, slice(border, T), vector_cols):
+            nc.vector.tensor_copy(out=pairs_of(cols)[:, 1, :, 1], in_=windows[D][:, cols])
+        for cols in (first_cols, late_cols, last_cols):
+            weave(nc.scalar.copy, U32, cols)
+        quantise_out(first_cols)
+        store_words(first_cols)
+        weave(nc.vector.tensor_copy, I32, vector_cols)
+        quantise_out(late_cols)
+        quantise_out(vector_cols)
+        store_words(vector_cols)
+        quantise_out(last_cols)
+        store_words(slice(border, T))
         for q in range(QUADS):
             queue = nc.sync if q % 2 == 0 else nc.scalar
             queue.dma_start(

@@ -24,7 +24,7 @@ CHUNKS = S // CHUNK
 PAIR = 2 * CHUNK
 SHARE_PASS0 = 80
 SHARE_PASS1 = (84, 48)
-WARM_PASSES = 2
+WARM_PASSES = 1
 A, B, C, D = range(PACK)
 QUARTER = T // 4
 

@@ -24,9 +24,9 @@ CHUNKS = S // CHUNK
 PAIR = 2 * CHUNK
 SHARE_PASS0 = 80
 SHARE_PASS1 = (84, 48)
-WARM_PASSES = 1
 A, B, C, D = range(PACK)
-QUARTER = T // 4
+ROW = T
+FIRST = 192
 
 
 def tile_picked_zmae_mlpgelu_po_kernel(
@@ -47,12 +47,12 @@ def tile_picked_zmae_mlpgelu_po_kernel(
 
         warm_in = tile("warm_in", [P, 8], F32)
         warm_out = tile("warm_out", [P, 8], F32)
-        x_scale_rows = tile("x_scale_rows", [P, T], U8)
         x_scale_table = tile("x_scale_table", [P, T], U8)
         w2_scale_raw = tile("w2_scale_raw", [P, N], U8)
-        nc.vector.memset(w2_scale_raw[:].bitcast(I32), 0)
-        nc.vector.memset(warm_in[:], 0.0)
         nc.vector.memset(x_scale_table[:].bitcast(I32), 0)
+        nc.vector.memset(warm_in[:], 0.0)
+        nc.vector.memset(w2_scale_raw[:].bitcast(I32), 0)
+        nc.scalar.activation(out=warm_out[:], in_=warm_in[:], func=GELU)
 
         w1_rows = w1.rearrange("(g p j) c -> g p j c", g=PASSES, j=PACK)
         w1_raw = [tile(f"w1_raw{g}", [P, PACK, H], F32) for g in range(PASSES)]
@@ -65,32 +65,24 @@ def tile_picked_zmae_mlpgelu_po_kernel(
         def load_x(g):
             nc.sync.dma_start(out=x_word_table[g][:], in_=x_words[g].rearrange("p c r -> p (c r)").bitcast(I32))
 
+        load_x(0)
         nc.sync.dma_start(offsets[:], offs)
         for q in range(QUADS):
-            queue = nc.sync if q < 2 else nc.scalar
-            queue.dma_start(
-                out=x_scale_rows[32 * q : 32 * q + 4 * PASSES, :].bitcast(I32),
+            nc.sync.dma_start(
+                out=x_scale_table[32 * q : 32 * q + 4 * PASSES, :].bitcast(I32),
                 in_=x_scales[:, 4 * q : 4 * q + 4, :].bitcast(I32),
             )
-        nc.scalar.activation(out=warm_out[:], in_=warm_in[:], func=GELU)
         nc.sync.dma_start(out=w1_raw[0][:], in_=w1_rows[0])
-        load_x(0)
-        nc.sync.dma_start(out=w1_raw[1][:], in_=w1_rows[1])
-        load_x(1)
-        nc.sync.dma_start(out=w2_word_raw[:], in_=w2_words[0].rearrange("p c r -> p (c r)").bitcast(I32))
         for q in range(QUADS):
             nc.sync.dma_start(
                 out=w2_scale_raw[32 * q : 32 * q + 4, :].bitcast(I32),
                 in_=w2_scales[0, 4 * q : 4 * q + 4, :].bitcast(I32),
             )
-        for t in range(PACK):
+        nc.sync.dma_start(out=w1_raw[1][:], in_=w1_rows[1])
+        load_x(1)
+        nc.sync.dma_start(out=w2_word_raw[:], in_=w2_words[0].rearrange("p c r -> p (c r)").bitcast(I32))
+        for t in (A, D, B, C):
             nc.sync.dma_start(out=windows[t][:], in_=mask_rows[t])
-
-        for q in range(QUADS):
-            live = slice(32 * q, 32 * q + 4 * PASSES)
-            nc.vector.tensor_copy(out=x_scale_table[live, :].bitcast(I32), in_=x_scale_rows[live, :].bitcast(I32))
-        x_scale = tile("x_scale", [P, S], U8)
-        nc.vector.tensor_copy(out=x_scale[:], in_=x_scale_table[:].indirect(offsets[:]))
 
         w1_bf = [tile(f"w1_bf{g}", [P, H * PACK], BF16) for g in range(PASSES)]
         w1_codes = [tile(f"w1_codes{g}", [P, H], U32) for g in range(PASSES)]
@@ -130,22 +122,14 @@ def tile_picked_zmae_mlpgelu_po_kernel(
                     stop=(g == PASSES - 1 and t == PACK - 1),
                 )
 
-        round_w1(0, slice(0, PACK), SHARE_PASS0)
-        quantise_w1(0, 0, H)
         x_first = tile("x_first", [P, S], U32)
         gather_words(x_first[:], 0, 0)
-        warm_ps = psum.tile([P, S], F32, name="warm_ps", tag="bank7")
-        for t in range(WARM_PASSES):
-            m = slice(t * P, (t + 1) * P)
-            nc.tensor.matmul_mx(
-                out=warm_ps[:],
-                lhsT=w1_codes[0][:, m].bitcast(FP8X4),
-                lhsT_scale=w1_scale[0][:, m],
-                rhs=w1_codes[0][:].bitcast(FP8X4),
-                rhs_scale=w1_scale[0][:],
-                start=True,
-                stop=True,
-            )
+        x_scale = tile("x_scale", [P, S], U8)
+        nc.vector.tensor_copy(out=x_scale[:], in_=x_scale_table[:].indirect(offsets[:]))
+        round_w1(0, slice(0, PACK), SHARE_PASS0)
+        quantise_w1(0, 0, H)
+        w2_scale = tile("w2_scale", [P, N], U8)
+        deal(nc.vector.tensor_copy, w2_scale[:], w2_scale_raw[:])
         for c in range(CHUNKS):
             first_layer(c, 0, x_first[:, c * CHUNK : (c + 1) * CHUNK])
         for u in range(2):
@@ -156,6 +140,7 @@ def tile_picked_zmae_mlpgelu_po_kernel(
             gather_words(x_early[:, u, :], 1, u * CHUNK)
 
         h_scale = tile("h_scale", [P, S], U8)
+        h_codes = tile("h_codes", [P, S], U32)
         w2_codes = tile("w2_codes", [P, N], I32)
 
         def gelu(c):
@@ -165,35 +150,42 @@ def tile_picked_zmae_mlpgelu_po_kernel(
                 func=GELU,
             )
 
-        def quantise_h(codes, first):
-            count = codes.shape[1]
+        def quantise_h(first, count):
+            cols = slice(first, first + count)
             values = h_bf[:, first * PACK : (first + count) * PACK]
-            nc.vector.quantize_mx(out=codes.bitcast(FP8X4), scales=h_scale[:, first : first + count], in_=values)
+            nc.vector.quantize_mx(out=h_codes[:, cols].bitcast(FP8X4), scales=h_scale[:, cols], in_=values)
 
-        def second_layer(y_ps, t, codes, first):
-            m = slice(t * P, (t + 1) * P)
-            nc.tensor.matmul_mx(
-                out=y_ps,
-                lhsT=w2_codes[:, m].bitcast(FP8X4),
-                lhsT_scale=w2_scale[:, m],
-                rhs=codes.bitcast(FP8X4),
-                rhs_scale=h_scale[:, first : first + codes.shape[1]],
-                start=True,
-                stop=True,
-            )
+        def second_layer(bank, tiles, first, count):
+            y_ps = psum.tile([P, len(tiles), count], F32, name=f"y_ps{tiles[0]}_{first}", tag=f"bank{bank}")
+            cols = slice(first, first + count)
+            for i, t in enumerate(tiles):
+                m = slice(t * P, (t + 1) * P)
+                nc.tensor.matmul_mx(
+                    out=y_ps[:, i, :],
+                    lhsT=w2_codes[:, m].bitcast(FP8X4),
+                    lhsT_scale=w2_scale[:, m],
+                    rhs=h_codes[:, cols].bitcast(FP8X4),
+                    rhs_scale=h_scale[:, cols],
+                    start=True,
+                    stop=True,
+                )
+            return y_ps
 
-        def vector_scatter(t, first, y):
-            nc.vector.tensor_copy(out=windows[t][:].indirect(picks(first, y.shape[1])), in_=y)
+        stage = tile("stage", [P, PACK * ROW], F32)
 
-        def scalar_scatter(t, first, y):
-            nc.scalar.activation(out=windows[t][:].indirect(picks(first, y.shape[1])), in_=y, func=COPY)
+        def place(t, first):
+            if first == 0 and t in (B, D):
+                first = PAIR
+            return t * ROW + FIRST + first
 
-        def product(copy, bank, t, first, y):
-            count = y.shape[1]
-            y_ps = psum.tile([P, count], F32, name=f"y_ps{t}_{first}", tag=f"bank{bank}")
-            codes = h_codes[:, first : first + count] if first < PAIR else late_codes[:]
-            second_layer(y_ps[:], t, codes, first)
-            copy(out=y, in_=y_ps[:])
+        def y_of(t, first, count):
+            return stage[:, place(t, first) : place(t, first) + count]
+
+        def vector_scatter(t, first, count):
+            nc.vector.tensor_copy(out=windows[t][:].indirect(picks(first, count)), in_=y_of(t, first, count))
+
+        def scalar_scatter(t, first, count):
+            nc.scalar.activation(out=windows[t][:].indirect(picks(first, count)), in_=y_of(t, first, count), func=COPY)
 
         deal(nc.scalar.copy, w2_codes[:].bitcast(U32), w2_word_raw[:].bitcast(U32))
         h_bf = tile("h_bf", [P, S * PACK], BF16, tag="w2_word_raw")
@@ -202,66 +194,54 @@ def tile_picked_zmae_mlpgelu_po_kernel(
             gelu(c)
         x_late = tile("x_late", [P, PAIR], U32)
         gather_words(x_late[:], 1, PAIR)
-        w2_scale = tile("w2_scale", [P, N], U8)
-        deal(nc.vector.tensor_copy, w2_scale[:], w2_scale_raw[:])
-        h_codes = tile("h_codes", [P, PAIR], U32, tag="w2_scale_raw")
-        quantise_h(h_codes[:, :CHUNK], 0)
-        a0, a1 = (tile(f"a{i}", [P, CHUNK], F32) for i in range(2))
-        a2, b0, b1, d0, d1 = (tile(name, [P, PAIR], F32) for name in ("a2", "b0", "b1", "d0", "d1"))
-        c_all = tile("c_all", [P, S], F32)
-        product(nc.vector.tensor_copy, 4, A, 0, a0[:])
-        quantise_h(h_codes[:, CHUNK:PAIR], CHUNK)
-        vector_scatter(A, 0, a0[:])
+        quantise_h(0, CHUNK)
+        ab0 = second_layer(4, (A, B), 0, CHUNK)
         for c in range(2):
             first_layer(2 + c, 1, x_late[:, c * CHUNK : (c + 1) * CHUNK])
             gelu(2 + c)
-        product(nc.scalar.copy, 5, A, CHUNK, a1[:])
-        product(nc.scalar.copy, 6, B, 0, b0[:])
-        product(nc.scalar.copy, 7, D, 0, d0[:])
-        product(nc.vector.tensor_copy, 0, C, 0, c_all[:, :PAIR])
-        late_codes = tile("late_codes", [P, PAIR], U32, tag="a0")
-        quantise_h(late_codes[:], PAIR)
-        vector_scatter(A, CHUNK, a1[:])
-        scalar_scatter(B, 0, b0[:])
-        product(nc.vector.tensor_copy, 1, A, PAIR, a2[:])
-        product(nc.vector.tensor_copy, 4, C, PAIR, c_all[:, PAIR:])
-        product(nc.scalar.copy, 2, B, PAIR, b1[:])
-        product(nc.scalar.copy, 3, D, PAIR, d1[:])
+        quantise_h(CHUNK, CHUNK)
+        all1 = second_layer(5, (A, B, C, D), CHUNK, CHUNK)
+        cd0 = second_layer(6, (C, D), 0, CHUNK)
+        nc.vector.tensor_copy(out=y_of(A, 0, CHUNK), in_=ab0[:, 0, :])
+        nc.vector.tensor_copy(out=y_of(B, 0, CHUNK), in_=ab0[:, 1, :])
+        vector_scatter(A, 0, CHUNK)
+        quantise_h(PAIR, PAIR)
+        rows = stage[:].rearrange("p (t c) -> p t c", t=PACK)
+        nc.scalar.copy(out=rows[:, :, FIRST + CHUNK : FIRST + PAIR], in_=all1[:])
+        step = place(D, 0) - place(C, 0)
+        nc.scalar.copy(out=stage[:, place(D, 0) + CHUNK - 2 * step : place(D, 0) + CHUNK].rearrange("p (u c) -> p u c", u=2)[:, :, step - CHUNK :], in_=cd0[:])
+        vector_scatter(A, CHUNK, CHUNK)
+        ac2 = second_layer(5, (A, C), PAIR, PAIR)
+        bd2 = second_layer(7, (B, D), PAIR, PAIR)
+        scalar_scatter(B, 0, CHUNK)
+        scalar_scatter(D, 0, CHUNK)
+        nc.vector.tensor_copy(out=y_of(A, PAIR, PAIR), in_=ac2[:, 0, :])
+        nc.vector.tensor_copy(out=y_of(C, PAIR, PAIR), in_=ac2[:, 1, :])
+        nc.scalar.copy(out=y_of(B, PAIR, PAIR), in_=bd2[:, 0, :])
+        nc.scalar.copy(out=y_of(D, PAIR, PAIR), in_=bd2[:, 1, :])
 
-        pairs = tile("pairs", [P, 2, T - QUARTER, 2], BF16)
+        pairs = stage[:].bitcast(BF16).rearrange("p (u r c e) -> p u r c e", u=2, r=2, e=2)[:, :, 0]
+        pair_words = stage[:].rearrange("p (u r c) -> p u r c", u=2, r=2)[:, :, 0]
         rounded = tile("rounded", [P, T, PACK], BF16)
         rounded_words = rounded[:].rearrange("p c t -> p (c t)").bitcast(U32).rearrange("p (c u) -> p c u", u=2)
-        quarter = [slice(i * QUARTER, (i + 1) * QUARTER) for i in range(4)]
 
         def store(t):
             nc.sync.dma_start(out=out_rows[t], in_=windows[t][:])
 
         def pool_round(t):
-            nc.gpsimd.tensor_scalar(
-                pairs[:, t // 2, :, t % 2], windows[t][:, QUARTER:], 1.0, -0.0, mybir.AluOpType.mult, mybir.AluOpType.add
-            )
+            nc.gpsimd.tensor_scalar(pairs[:, 0, :, t], windows[t][:], 1.0, -0.0, mybir.AluOpType.mult, mybir.AluOpType.add)
 
-        vector_scatter(A, PAIR, a2[:])
+        vector_scatter(A, PAIR, PAIR)
         store(A)
         pool_round(A)
-        scalar_scatter(B, PAIR, b1[:])
+        scalar_scatter(B, CHUNK, S - CHUNK)
         store(B)
         pool_round(B)
-        vector_scatter(C, 0, c_all[:])
+        vector_scatter(C, 0, S)
         store(C)
-        nc.vector.tensor_copy(out=pairs[:, 1, :, 0], in_=windows[C][:, QUARTER:])
-        scalar_scatter(D, 0, d0[:])
-        scalar_scatter(D, PAIR, d1[:])
+        nc.vector.tensor_copy(out=pairs[:, 1, :, 0], in_=windows[C][:])
+        scalar_scatter(D, CHUNK, S - CHUNK)
         store(D)
-        first_pairs = tile("first_pairs", [P, 2, QUARTER, 2], BF16, tag="d0")
-        for t in (A, B):
-            nc.scalar.copy(out=first_pairs[:, 0, :, t], in_=windows[t][:, :QUARTER])
-        nc.vector.tensor_copy(out=first_pairs[:, 1, :, 0], in_=windows[C][:, :QUARTER])
-
-        def pairs_of(cols):
-            if cols.start < QUARTER:
-                return first_pairs[:, :, cols, :]
-            return pairs[:, :, cols.start - QUARTER : cols.stop - QUARTER, :]
 
         out_codes = tile("out_codes", [P, T], I32)
         out_scale = tile("out_scale", [P, T], U8)
@@ -275,26 +255,25 @@ def tile_picked_zmae_mlpgelu_po_kernel(
             )
 
         def weave(copy, dtype, cols):
-            copy(out=rounded_words[:, cols, :].bitcast(dtype), in_=pairs_of(cols).rearrange("p u c e -> p u (c e)").bitcast(dtype).rearrange("p u c -> p c u"))
+            copy(out=rounded_words[:, cols, :].bitcast(dtype), in_=pair_words[:, :, cols].bitcast(dtype).rearrange("p u c -> p c u"))
 
         def store_words(cols):
             nc.sync.dma_start(out=out_words[:, cols], in_=out_codes[:, cols])
 
-        border = 2 * QUARTER + CHUNK
-        first_cols, vector_cols = quarter[0], slice(QUARTER, border)
-        late_cols, last_cols = slice(border, T - CHUNK), slice(T - CHUNK, T)
-        for cols in (first_cols, slice(border, T), vector_cols):
-            nc.vector.tensor_copy(out=pairs_of(cols)[:, 1, :, 1], in_=windows[D][:, cols])
+        first_cols, vector_cols = slice(0, PAIR), slice(PAIR, 5 * CHUNK)
+        late_cols, last_cols = slice(5 * CHUNK, 7 * CHUNK), slice(7 * CHUNK, T)
+        for cols in (first_cols, vector_cols, slice(5 * CHUNK, T)):
+            nc.vector.tensor_copy(out=pairs[:, 1, cols, 1], in_=windows[D][:, cols])
         for cols in (first_cols, late_cols, last_cols):
             weave(nc.scalar.copy, U32, cols)
+        weave(nc.vector.tensor_copy, I32, vector_cols)
         quantise_out(first_cols)
         store_words(first_cols)
-        weave(nc.vector.tensor_copy, I32, vector_cols)
-        quantise_out(late_cols)
         quantise_out(vector_cols)
         store_words(vector_cols)
+        quantise_out(late_cols)
         quantise_out(last_cols)
-        store_words(slice(border, T))
+        store_words(slice(5 * CHUNK, T))
         for q in range(QUADS):
             queue = nc.sync if q % 2 == 0 else nc.scalar
             queue.dma_start(

@@ -47,12 +47,15 @@ def tile_picked_zmae_mlpgelu_po_kernel(
 
         warm_in = tile("warm_in", [P, 8], F32)
         warm_out = tile("warm_out", [P, 8], F32)
+        x_scale_rows = tile("x_scale_rows", [P, T], U8)
         x_scale_table = tile("x_scale_table", [P, T], U8)
         w2_scale_raw = tile("w2_scale_raw", [P, N], U8)
         nc.vector.memset(x_scale_table[:].bitcast(I32), 0)
         nc.vector.memset(warm_in[:], 0.0)
         nc.vector.memset(w2_scale_raw[:].bitcast(I32), 0)
-        nc.scalar.activation(out=warm_out[:], in_=warm_in[:], func=GELU)
+        stage = tile("stage", [P, PACK * ROW], F32)
+        one = stage[:].bitcast(BF16)[:, 1:2]
+        nc.vector.memset(one, 1.0)
 
         w1_rows = w1.rearrange("(g p j) c -> g p j c", g=PASSES, j=PACK)
         w1_raw = [tile(f"w1_raw{g}", [P, PACK, H], F32) for g in range(PASSES)]
@@ -65,21 +68,23 @@ def tile_picked_zmae_mlpgelu_po_kernel(
         def load_x(g):
             nc.sync.dma_start(out=x_word_table[g][:], in_=x_words[g].rearrange("p c r -> p (c r)").bitcast(I32))
 
-        load_x(0)
         nc.sync.dma_start(offsets[:], offs)
         for q in range(QUADS):
-            nc.sync.dma_start(
-                out=x_scale_table[32 * q : 32 * q + 4 * PASSES, :].bitcast(I32),
+            queue = nc.sync if q < 2 else nc.scalar
+            queue.dma_start(
+                out=x_scale_rows[32 * q : 32 * q + 4 * PASSES, :].bitcast(I32),
                 in_=x_scales[:, 4 * q : 4 * q + 4, :].bitcast(I32),
             )
+        nc.scalar.activation(out=warm_out[:], in_=warm_in[:], func=GELU)
         nc.sync.dma_start(out=w1_raw[0][:], in_=w1_rows[0])
+        load_x(0)
+        nc.sync.dma_start(out=w1_raw[1][:], in_=w1_rows[1])
+        load_x(1)
         for q in range(QUADS):
             nc.sync.dma_start(
                 out=w2_scale_raw[32 * q : 32 * q + 4, :].bitcast(I32),
                 in_=w2_scales[0, 4 * q : 4 * q + 4, :].bitcast(I32),
             )
-        nc.sync.dma_start(out=w1_raw[1][:], in_=w1_rows[1])
-        load_x(1)
         nc.sync.dma_start(out=w2_word_raw[:], in_=w2_words[0].rearrange("p c r -> p (c r)").bitcast(I32))
         for t in (A, D, B, C):
             nc.sync.dma_start(out=windows[t][:], in_=mask_rows[t])
@@ -122,14 +127,25 @@ def tile_picked_zmae_mlpgelu_po_kernel(
                     stop=(g == PASSES - 1 and t == PACK - 1),
                 )
 
-        x_first = tile("x_first", [P, S], U32)
-        gather_words(x_first[:], 0, 0)
+        for q in range(QUADS):
+            live = slice(32 * q, 32 * q + 4 * PASSES)
+            nc.vector.tensor_copy(out=x_scale_table[live, :].bitcast(I32), in_=x_scale_rows[live, :].bitcast(I32))
         x_scale = tile("x_scale", [P, S], U8)
         nc.vector.tensor_copy(out=x_scale[:], in_=x_scale_table[:].indirect(offsets[:]))
         round_w1(0, slice(0, PACK), SHARE_PASS0)
         quantise_w1(0, 0, H)
-        w2_scale = tile("w2_scale", [P, N], U8)
-        deal(nc.vector.tensor_copy, w2_scale[:], w2_scale_raw[:])
+        x_first = tile("x_first", [P, S], U32)
+        gather_words(x_first[:], 0, 0)
+        warm_ps = psum.tile([P, S], F32, name="warm_ps", tag="bank7")
+        nc.tensor.matmul_mx(
+            out=warm_ps[:],
+            lhsT=w1_codes[0][:, :P].bitcast(FP8X4),
+            lhsT_scale=w1_scale[0][:, :P],
+            rhs=w1_codes[0][:].bitcast(FP8X4),
+            rhs_scale=w1_scale[0][:],
+            start=True,
+            stop=True,
+        )
         for c in range(CHUNKS):
             first_layer(c, 0, x_first[:, c * CHUNK : (c + 1) * CHUNK])
         for u in range(2):
@@ -171,7 +187,6 @@ def tile_picked_zmae_mlpgelu_po_kernel(
                 )
             return y_ps
 
-        stage = tile("stage", [P, PACK * ROW], F32)
 
         def place(t, first):
             if first == 0 and t in (B, D):
@@ -194,16 +209,19 @@ def tile_picked_zmae_mlpgelu_po_kernel(
             gelu(c)
         x_late = tile("x_late", [P, PAIR], U32)
         gather_words(x_late[:], 1, PAIR)
+        w2_scale = tile("w2_scale", [P, N], U8)
+        deal(nc.vector.tensor_copy, w2_scale[:], w2_scale_raw[:])
         quantise_h(0, CHUNK)
-        ab0 = second_layer(4, (A, B), 0, CHUNK)
+        a0 = second_layer(4, (A,), 0, CHUNK)
+        b0 = second_layer(0, (B,), 0, CHUNK)
         for c in range(2):
             first_layer(2 + c, 1, x_late[:, c * CHUNK : (c + 1) * CHUNK])
             gelu(2 + c)
         quantise_h(CHUNK, CHUNK)
         all1 = second_layer(5, (A, B, C, D), CHUNK, CHUNK)
         cd0 = second_layer(6, (C, D), 0, CHUNK)
-        nc.vector.tensor_copy(out=y_of(A, 0, CHUNK), in_=ab0[:, 0, :])
-        nc.vector.tensor_copy(out=y_of(B, 0, CHUNK), in_=ab0[:, 1, :])
+        nc.vector.tensor_copy(out=y_of(A, 0, CHUNK), in_=a0[:, 0, :])
+        nc.vector.tensor_copy(out=y_of(B, 0, CHUNK), in_=b0[:, 0, :])
         vector_scatter(A, 0, CHUNK)
         quantise_h(PAIR, PAIR)
         rows = stage[:].rearrange("p (t c) -> p t c", t=PACK)
@@ -228,17 +246,18 @@ def tile_picked_zmae_mlpgelu_po_kernel(
         def store(t):
             nc.sync.dma_start(out=out_rows[t], in_=windows[t][:])
 
-        def pool_round(t):
-            nc.gpsimd.tensor_scalar(pairs[:, 0, :, t], windows[t][:], 1.0, -0.0, mybir.AluOpType.mult, mybir.AluOpType.add)
+        def pool_round(t, cols, one):
+            nc.gpsimd.tensor_scalar(pairs[:, 0, cols, t], windows[t][:, cols], one, -0.0, mybir.AluOpType.mult, mybir.AluOpType.add)
 
         vector_scatter(A, PAIR, PAIR)
         store(A)
-        pool_round(A)
+        pool_round(A, slice(0, T), one)
         scalar_scatter(B, CHUNK, S - CHUNK)
         store(B)
-        pool_round(B)
+        pool_round(B, slice(PAIR, T), 1.0)
         vector_scatter(C, 0, S)
         store(C)
+        nc.vector.tensor_copy(out=pairs[:, 0, :PAIR, B], in_=windows[B][:, :PAIR])
         nc.vector.tensor_copy(out=pairs[:, 1, :, 0], in_=windows[C][:])
         scalar_scatter(D, CHUNK, S - CHUNK)
         store(D)

@@ -13,6 +13,7 @@ U16 = mybir.dt.uint16
 U8 = mybir.dt.uint8
 FP8X4 = mybir.dt.float8_e4m3fn_x4
 GELU = mybir.ActivationFunctionType.Gelu_apprx_tanh
+IDENTITY = mybir.ActivationFunctionType.Identity
 COPY = mybir.ActivationFunctionType.Copy
 
 P = 128
@@ -25,7 +26,9 @@ PAIR = 2 * CHUNK
 SHARE_PASS0 = 80
 SHARE_PASS1 = (84, 48)
 A, B, C, D = range(PACK)
-ROW = T
+ROW = 696
+CD_PAIRS = 2096
+SPLIT_C = 704
 FIRST = 192
 
 
@@ -35,6 +38,7 @@ def tile_picked_zmae_mlpgelu_po_kernel(
     nc = tc.nc
     with ExitStack() as ctx:
         keep = ctx.enter_context(tc.tile_pool(name="keep", bufs=1))
+        shared = ctx.enter_context(tc.tile_pool(name="shared", bufs=1))
         psum = ctx.enter_context(tc.psum_pool(name="psum", bufs=1))
 
         def tile(name, shape, dtype, tag=None):
@@ -49,13 +53,15 @@ def tile_picked_zmae_mlpgelu_po_kernel(
         warm_out = tile("warm_out", [P, 8], F32)
         x_scale_rows = tile("x_scale_rows", [P, T], U8)
         x_scale_table = tile("x_scale_table", [P, T], U8)
-        w2_scale_raw = tile("w2_scale_raw", [P, N], U8)
+        w2_scale_raw = shared.tile([P, N], U8, name="w2_scale_raw", align_bytes=64, offset=4 * S - N // 2)
         nc.vector.memset(x_scale_table[:].bitcast(I32), 0)
         nc.vector.memset(warm_in[:], 0.0)
         nc.vector.memset(w2_scale_raw[:].bitcast(I32), 0)
-        stage = tile("stage", [P, PACK * ROW], F32)
+        stage = tile("stage", [P, 2 * CD_PAIRS], F32)
         one = stage[:].bitcast(BF16)[:, 1:2]
         nc.vector.memset(one, 1.0)
+        nothing = stage[:].bitcast(BF16)[:, 2 * (CD_PAIRS + T) - 1 : 2 * (CD_PAIRS + T)]
+        nc.vector.memset(nothing, -0.0)
 
         w1_rows = w1.rearrange("(g p j) c -> g p j c", g=PASSES, j=PACK)
         w1_raw = [tile(f"w1_raw{g}", [P, PACK, H], F32) for g in range(PASSES)]
@@ -80,12 +86,12 @@ def tile_picked_zmae_mlpgelu_po_kernel(
         load_x(0)
         nc.sync.dma_start(out=w1_raw[1][:], in_=w1_rows[1])
         load_x(1)
+        nc.sync.dma_start(out=w2_word_raw[:], in_=w2_words[0].rearrange("p c r -> p (c r)").bitcast(I32))
         for q in range(QUADS):
             nc.sync.dma_start(
                 out=w2_scale_raw[32 * q : 32 * q + 4, :].bitcast(I32),
                 in_=w2_scales[0, 4 * q : 4 * q + 4, :].bitcast(I32),
             )
-        nc.sync.dma_start(out=w2_word_raw[:], in_=w2_words[0].rearrange("p c r -> p (c r)").bitcast(I32))
         for t in (A, D, B, C):
             nc.sync.dma_start(out=windows[t][:], in_=mask_rows[t])
 
@@ -156,19 +162,21 @@ def tile_picked_zmae_mlpgelu_po_kernel(
             gather_words(x_early[:, u, :], 1, u * CHUNK)
 
         h_scale = tile("h_scale", [P, S], U8)
-        h_codes = tile("h_codes", [P, S], U32)
         w2_codes = tile("w2_codes", [P, N], I32)
+
+        def h_values(first, count):
+            return h_bf[first // PAIR][:, first % PAIR * PACK : (first % PAIR + count) * PACK]
 
         def gelu(c):
             nc.scalar.activation(
-                out=h_bf[:, c * CHUNK * PACK : (c + 1) * CHUNK * PACK].rearrange("p (n t) -> p n t", t=PACK),
+                out=h_values(c * CHUNK, CHUNK).rearrange("p (n t) -> p n t", t=PACK),
                 in_=h_ps[c][:].rearrange("p t n -> p n t"),
                 func=GELU,
             )
 
         def quantise_h(first, count):
             cols = slice(first, first + count)
-            values = h_bf[:, first * PACK : (first + count) * PACK]
+            values = h_values(first, count)
             nc.vector.quantize_mx(out=h_codes[:, cols].bitcast(FP8X4), scales=h_scale[:, cols], in_=values)
 
         def second_layer(bank, tiles, first, count):
@@ -191,7 +199,7 @@ def tile_picked_zmae_mlpgelu_po_kernel(
         def place(t, first):
             if first == 0 and t in (B, D):
                 first = PAIR
-            return t * ROW + FIRST + first
+            return (A, B, D, C).index(t) * ROW + FIRST + first
 
         def y_of(t, first, count):
             return stage[:, place(t, first) : place(t, first) + count]
@@ -203,7 +211,7 @@ def tile_picked_zmae_mlpgelu_po_kernel(
             nc.scalar.activation(out=windows[t][:].indirect(picks(first, count)), in_=y_of(t, first, count), func=COPY)
 
         deal(nc.scalar.copy, w2_codes[:].bitcast(U32), w2_word_raw[:].bitcast(U32))
-        h_bf = tile("h_bf", [P, S * PACK], BF16, tag="w2_word_raw")
+        h_bf = [tile("h_early", [P, PAIR * PACK], BF16, tag="w2_word_raw")]
         for c in range(2):
             first_layer(c, 1, x_early[:, c, :])
             gelu(c)
@@ -211,25 +219,25 @@ def tile_picked_zmae_mlpgelu_po_kernel(
         gather_words(x_late[:], 1, PAIR)
         w2_scale = tile("w2_scale", [P, N], U8)
         deal(nc.vector.tensor_copy, w2_scale[:], w2_scale_raw[:])
+        h_codes = shared.tile([P, S], U32, name="h_codes", align_bytes=64, offset=0)
+        h_bf.append(shared.tile([P, PAIR * PACK], BF16, name="h_late", align_bytes=64, offset=4 * S))
         quantise_h(0, CHUNK)
-        a0 = second_layer(4, (A,), 0, CHUNK)
-        b0 = second_layer(0, (B,), 0, CHUNK)
+        ac0 = second_layer(4, (A, C), 0, CHUNK)
+        bd0 = second_layer(0, (B, D), 0, CHUNK)
         for c in range(2):
             first_layer(2 + c, 1, x_late[:, c * CHUNK : (c + 1) * CHUNK])
             gelu(2 + c)
         quantise_h(CHUNK, CHUNK)
-        all1 = second_layer(5, (A, B, C, D), CHUNK, CHUNK)
-        cd0 = second_layer(6, (C, D), 0, CHUNK)
-        nc.vector.tensor_copy(out=y_of(A, 0, CHUNK), in_=a0[:, 0, :])
-        nc.vector.tensor_copy(out=y_of(B, 0, CHUNK), in_=b0[:, 0, :])
-        vector_scatter(A, 0, CHUNK)
+        a1 = second_layer(6, (A,), CHUNK, CHUNK)
+        bdc1 = second_layer(5, (B, D, C), CHUNK, CHUNK)
+        rows = stage[:, : PACK * ROW].rearrange("p (t c) -> p t c", t=PACK)
+        nc.vector.tensor_copy(out=rows[:, ::3, FIRST : FIRST + CHUNK], in_=ac0[:])
+        nc.vector.tensor_copy(out=rows[:, 1:3, FIRST + PAIR : FIRST + PAIR + CHUNK], in_=bd0[:])
+        nc.vector.tensor_copy(out=y_of(A, CHUNK, CHUNK), in_=a1[:, 0, :])
         quantise_h(PAIR, PAIR)
-        rows = stage[:].rearrange("p (t c) -> p t c", t=PACK)
-        nc.scalar.copy(out=rows[:, :, FIRST + CHUNK : FIRST + PAIR], in_=all1[:])
-        step = place(D, 0) - place(C, 0)
-        nc.scalar.copy(out=stage[:, place(D, 0) + CHUNK - 2 * step : place(D, 0) + CHUNK].rearrange("p (u c) -> p u c", u=2)[:, :, step - CHUNK :], in_=cd0[:])
-        vector_scatter(A, CHUNK, CHUNK)
-        ac2 = second_layer(5, (A, C), PAIR, PAIR)
+        nc.scalar.copy(out=rows[:, 1:, FIRST + CHUNK : FIRST + PAIR], in_=bdc1[:])
+        vector_scatter(A, 0, PAIR)
+        ac2 = second_layer(4, (A, C), PAIR, PAIR)
         bd2 = second_layer(7, (B, D), PAIR, PAIR)
         scalar_scatter(B, 0, CHUNK)
         scalar_scatter(D, 0, CHUNK)
@@ -238,8 +246,8 @@ def tile_picked_zmae_mlpgelu_po_kernel(
         nc.scalar.copy(out=y_of(B, PAIR, PAIR), in_=bd2[:, 0, :])
         nc.scalar.copy(out=y_of(D, PAIR, PAIR), in_=bd2[:, 1, :])
 
-        pairs = stage[:].bitcast(BF16).rearrange("p (u r c e) -> p u r c e", u=2, r=2, e=2)[:, :, 0]
-        pair_words = stage[:].rearrange("p (u r c) -> p u r c", u=2, r=2)[:, :, 0]
+        pairs = stage[:].bitcast(BF16).rearrange("p (u c e) -> p u c e", u=2, e=2)[:, :, :T]
+        pair_words = stage[:].rearrange("p (u c) -> p u c", u=2)[:, :, :T]
         rounded = tile("rounded", [P, T, PACK], BF16)
         rounded_words = rounded[:].rearrange("p c t -> p (c t)").bitcast(U32).rearrange("p (c u) -> p c u", u=2)
 
@@ -251,16 +259,19 @@ def tile_picked_zmae_mlpgelu_po_kernel(
 
         vector_scatter(A, PAIR, PAIR)
         store(A)
-        pool_round(A, slice(0, T), one)
+        pool_round(A, slice(0, T - CHUNK), one)
         scalar_scatter(B, CHUNK, S - CHUNK)
         store(B)
-        pool_round(B, slice(PAIR, T), 1.0)
+        pool_round(B, slice(PAIR, T - CHUNK), 1.0)
         vector_scatter(C, 0, S)
         store(C)
         nc.vector.tensor_copy(out=pairs[:, 0, :PAIR, B], in_=windows[B][:, :PAIR])
-        nc.vector.tensor_copy(out=pairs[:, 1, :, 0], in_=windows[C][:])
+        nc.vector.tensor_copy(out=pairs[:, 1, :SPLIT_C, 0], in_=windows[C][:, :SPLIT_C])
         scalar_scatter(D, CHUNK, S - CHUNK)
         store(D)
+        nc.scalar.activation(out=pairs[:, 1, SPLIT_C:, 0], in_=windows[C][:, SPLIT_C:], func=IDENTITY, bias=nothing)
+        for t in (A, B):
+            nc.scalar.copy(out=pairs[:, 0, T - CHUNK :, t], in_=windows[t][:, T - CHUNK :])
 
         out_codes = tile("out_codes", [P, T], I32)
         out_scale = tile("out_scale", [P, T], U8)

@@ -23,12 +23,11 @@ QUADS = 4
 CHUNK = 128
 CHUNKS = S // CHUNK
 PAIR = 2 * CHUNK
-SHARE_PASS0 = 80
 SHARE_PASS1 = (84, 48)
 A, B, C, D = range(PACK)
 ROW = 696
 CD_PAIRS = 2096
-SPLIT_C = 704
+SPLIT_C = 640
 FIRST = 192
 
 
@@ -82,8 +81,8 @@ def tile_picked_zmae_mlpgelu_po_kernel(
                 in_=x_scales[:, 4 * q : 4 * q + 4, :].bitcast(I32),
             )
         nc.scalar.activation(out=warm_out[:], in_=warm_in[:], func=GELU)
-        nc.sync.dma_start(out=w1_raw[0][:], in_=w1_rows[0])
         load_x(0)
+        nc.sync.dma_start(out=w1_raw[0][:], in_=w1_rows[0])
         nc.sync.dma_start(out=w1_raw[1][:], in_=w1_rows[1])
         load_x(1)
         nc.sync.dma_start(out=w2_word_raw[:], in_=w2_words[0].rearrange("p c r -> p (c r)").bitcast(I32))
@@ -100,9 +99,13 @@ def tile_picked_zmae_mlpgelu_po_kernel(
         w1_scale = [tile(f"w1_scale{g}", [P, H], U8) for g in range(PASSES)]
         h_ps = [psum.tile([P, PACK, CHUNK], F32, name=f"h_ps{c}", tag=f"bank{c}") for c in range(CHUNKS)]
 
-        def round_w1(g, tiles, share):
+        def w1_views(g, tiles):
             src = w1_raw[g][:].rearrange("p j (m t) -> p m j t", t=PACK)[:, :, :, tiles]
             dst = w1_bf[g][:].rearrange("p (t m j) -> p m j t", t=PACK, j=PACK)[:, :, :, tiles]
+            return src, dst
+
+        def round_w1(g, tiles, share):
+            src, dst = w1_views(g, tiles)
             nc.vector.tensor_copy(out=dst[:, :share], in_=src[:, :share])
             nc.scalar.copy(out=dst[:, share:], in_=src[:, share:])
 
@@ -120,8 +123,8 @@ def tile_picked_zmae_mlpgelu_po_kernel(
         def gather_words(codes, g, first):
             nc.vector.tensor_copy(out=codes, in_=x_word_table[g][:].bitcast(U32).indirect(picks(first, codes.shape[1])))
 
-        def first_layer(c, g, codes):
-            for t in range(PACK):
+        def first_layer(c, g, codes, tiles=range(PACK)):
+            for t in tiles:
                 m = slice(t * P, (t + 1) * P)
                 nc.tensor.matmul_mx(
                     out=h_ps[c][:, t, :],
@@ -138,22 +141,15 @@ def tile_picked_zmae_mlpgelu_po_kernel(
             nc.vector.tensor_copy(out=x_scale_table[live, :].bitcast(I32), in_=x_scale_rows[live, :].bitcast(I32))
         x_scale = tile("x_scale", [P, S], U8)
         nc.vector.tensor_copy(out=x_scale[:], in_=x_scale_table[:].indirect(offsets[:]))
-        round_w1(0, slice(0, PACK), SHARE_PASS0)
-        quantise_w1(0, 0, H)
         x_first = tile("x_first", [P, S], U32)
         gather_words(x_first[:], 0, 0)
-        warm_ps = psum.tile([P, S], F32, name="warm_ps", tag="bank7")
-        nc.tensor.matmul_mx(
-            out=warm_ps[:],
-            lhsT=w1_codes[0][:, :P].bitcast(FP8X4),
-            lhsT_scale=w1_scale[0][:, :P],
-            rhs=w1_codes[0][:].bitcast(FP8X4),
-            rhs_scale=w1_scale[0][:],
-            start=True,
-            stop=True,
-        )
-        for c in range(CHUNKS):
-            first_layer(c, 0, x_first[:, c * CHUNK : (c + 1) * CHUNK])
+        for u, copy in enumerate((nc.vector.tensor_copy, nc.scalar.copy)):
+            src, dst = w1_views(0, slice(2 * u, 2 * u + 2))
+            copy(out=dst, in_=src)
+        for u in range(2):
+            quantise_w1(0, u * H // 2, H // 2)
+            for c in range(CHUNKS):
+                first_layer(c, 0, x_first[:, c * CHUNK : (c + 1) * CHUNK], range(2 * u, 2 * u + 2))
         for u in range(2):
             round_w1(1, slice(2 * u, 2 * u + 2), SHARE_PASS1[u])
         x_early = tile("x_early", [P, 2, CHUNK], U32)

from contextlib import ExitStack

import concourse.mybir as mybir

K, T, S, H, N = 1024, 1024, 512, 512, 512
FLOPS = 2 * K * H * S + 2 * H * N * S

F32 = mybir.dt.float32
BF16 = mybir.dt.bfloat16
I32 = mybir.dt.int32
U32 = mybir.dt.uint32
U16 = mybir.dt.uint16
U8 = mybir.dt.uint8
FP8X4 = mybir.dt.float8_e4m3fn_x4
GELU = mybir.ActivationFunctionType.Gelu_apprx_tanh
IDENTITY = mybir.ActivationFunctionType.Identity
COPY = mybir.ActivationFunctionType.Copy

P = 128
PACK = 4
PASSES = K // (P * PACK)
QUADS = 4
CHUNK = 128
CHUNKS = S // CHUNK
PAIR = 2 * CHUNK
SHARE_PASS1 = (84, 48)
A, B, C, D = range(PACK)
ROW = 696
CD_PAIRS = 2096
SPLIT_C = 640
FIRST = 192


def tile_picked_zmae_mlpgelu_po_kernel(
    tc, x_words, x_scales, mask, w1, w2_words, w2_scales, offs, out_0, out_1, out_2
):
    nc = tc.nc
    with ExitStack() as ctx:
        keep = ctx.enter_context(tc.tile_pool(name="keep", bufs=1))
        shared = ctx.enter_context(tc.tile_pool(name="shared", bufs=1))
        psum = ctx.enter_context(tc.psum_pool(name="psum", bufs=1))

        def tile(name, shape, dtype, tag=None):
            return keep.tile(shape, dtype, name=name, tag=tag or name, align_bytes=64)

        offsets = keep.tile([P, S // 16], U16, name="offsets")

        def picks(first, count):
            return offsets[:, first // 16 : (first + count) // 16]

        warm_in = tile("warm_in", [P, 8], F32)
        warm_out = tile("warm_out", [P, 8], F32)
        x_scale_rows = tile("x_scale_rows", [P, T], U8)
        x_scale_table = tile("x_scale_table", [P, T], U8)
        w2_scale_raw = shared.tile([P, N], U8, name="w2_scale_raw", align_bytes=64, offset=4 * S - N // 2)
        nc.vector.memset(x_scale_table[:].bitcast(I32), 0)
        nc.vector.memset(warm_in[:], 0.0)
        nc.vector.memset(w2_scale_raw[:].bitcast(I32), 0)
        stage = tile("stage", [P, 2 * CD_PAIRS], F32)
        one = stage[:].bitcast(BF16)[:, 1:2]
        nc.vector.memset(one, 1.0)
        nothing = stage[:].bitcast(BF16)[:, 2 * (CD_PAIRS + T) - 1 : 2 * (CD_PAIRS + T)]
        nc.vector.memset(nothing, -0.0)

        w1_rows = w1.rearrange("(g p j) c -> g p j c", g=PASSES, j=PACK)
        w1_raw = [tile(f"w1_raw{g}", [P, PACK, H], F32) for g in range(PASSES)]
        x_word_table = [tile(f"x_word_table{g}", [P, T], I32) for g in range(PASSES)]
        w2_word_raw = tile("w2_word_raw", [P, N], I32)
        windows = [tile(f"window{t}", [P, T], F32) for t in range(PACK)]
        mask_rows = mask.rearrange("(p t) c -> t p c", t=PACK)
        out_rows = out_0.rearrange("(p t) c -> t p c", t=PACK)

        def load_x(g):
            nc.sync.dma_start(out=x_word_table[g][:], in_=x_words[g].rearrange("p c r -> p (c r)").bitcast(I32))

        nc.sync.dma_start(offsets[:], offs)
        for q in range(QUADS):
            queue = nc.sync if q < 2 else nc.scalar
            queue.dma_start(
                out=x_scale_rows[32 * q : 32 * q + 4 * PASSES, :].bitcast(I32),
                in_=x_scales[:, 4 * q : 4 * q + 4, :].bitcast(I32),
            )
        nc.scalar.activation(out=warm_out[:], in_=warm_in[:], func=GELU)
        load_x(0)
        nc.sync.dma_start(out=w1_raw[0][:], in_=w1_rows[0])
        nc.sync.dma_start(out=w1_raw[1][:], in_=w1_rows[1])
        load_x(1)
        nc.sync.dma_start(out=w2_word_raw[:], in_=w2_words[0].rearrange("p c r -> p (c r)").bitcast(I32))
        for q in range(QUADS):
            nc.sync.dma_start(
                out=w2_scale_raw[32 * q : 32 * q + 4, :].bitcast(I32),
                in_=w2_scales[0, 4 * q : 4 * q + 4, :].bitcast(I32),
            )
        for t in (A, D, B, C):
            nc.sync.dma_start(out=windows[t][:], in_=mask_rows[t])

        w1_bf = [tile(f"w1_bf{g}", [P, H * PACK], BF16) for g in range(PASSES)]
        w1_codes = [tile(f"w1_codes{g}", [P, H], U32) for g in range(PASSES)]
        w1_scale = [tile(f"w1_scale{g}", [P, H], U8) for g in range(PASSES)]
        h_ps = [psum.tile([P, PACK, CHUNK], F32, name=f"h_ps{c}", tag=f"bank{c}") for c in range(CHUNKS)]

        def w1_views(g, tiles):
            src = w1_raw[g][:].rearrange("p j (m t) -> p m j t", t=PACK)[:, :, :, tiles]
            dst = w1_bf[g][:].rearrange("p (t m j) -> p m j t", t=PACK, j=PACK)[:, :, :, tiles]
            return src, dst

        def round_w1(g, tiles, share):
            src, dst = w1_views(g, tiles)
            nc.vector.tensor_copy(out=dst[:, :share], in_=src[:, :share])
            nc.scalar.copy(out=dst[:, share:], in_=src[:, share:])

        def deal(copy, dealt, raw):
            copy(out=dealt.rearrange("p (t m) -> p m t", t=PACK), in_=raw.rearrange("p (m t) -> p m t", t=PACK))

        def quantise_w1(g, first, count):
            cols = slice(first, first + count)
            nc.vector.quantize_mx(
                out=w1_codes[g][:, cols].bitcast(FP8X4),
                scales=w1_scale[g][:, cols],
                in_=w1_bf[g][:, PACK * first : PACK * (first + count)],
            )

        def gather_words(codes, g, first):
            nc.vector.tensor_copy(out=codes, in_=x_word_table[g][:].bitcast(U32).indirect(picks(first, codes.shape[1])))

        def first_layer(c, g, codes, tiles=range(PACK)):
            for t in tiles:
                m = slice(t * P, (t + 1) * P)
                nc.tensor.matmul_mx(
                    out=h_ps[c][:, t, :],
                    lhsT=w1_codes[g][:, m].bitcast(FP8X4),
                    lhsT_scale=w1_scale[g][:, m],
                    rhs=codes.bitcast(FP8X4),
                    rhs_scale=x_scale[4 * g :, c * CHUNK : (c + 1) * CHUNK],
                    start=(g == 0 and t == 0),
                    stop=(g == PASSES - 1 and t == PACK - 1),
                )

        for q in range(QUADS):
            live = slice(32 * q, 32 * q + 4 * PASSES)
            nc.vector.tensor_copy(out=x_scale_table[live, :].bitcast(I32), in_=x_scale_rows[live, :].bitcast(I32))
        x_scale = tile("x_scale", [P, S], U8)
        nc.vector.tensor_copy(out=x_scale[:], in_=x_scale_table[:].indirect(offsets[:]))
        x_first = tile("x_first", [P, S], U32)
        gather_words(x_first[:], 0, 0)
        for u, copy in enumerate((nc.vector.tensor_copy, nc.scalar.copy)):
            src, dst = w1_views(0, slice(2 * u, 2 * u + 2))
            copy(out=dst, in_=src)
        for u in range(2):
            quantise_w1(0, u * H // 2, H // 2)
            for c in range(CHUNKS):
                first_layer(c, 0, x_first[:, c * CHUNK : (c + 1) * CHUNK], range(2 * u, 2 * u + 2))
        for u in range(2):
            round_w1(1, slice(2 * u, 2 * u + 2), SHARE_PASS1[u])
        x_early = tile("x_early", [P, 2, CHUNK], U32)
        for u in range(2):
            quantise_w1(1, u * H // 2, H // 2)
            gather_words(x_early[:, u, :], 1, u * CHUNK)

        h_scale = tile("h_scale", [P, S], U8)
        w2_codes = tile("w2_codes", [P, N], I32)

        def h_values(first, count):
            return h_bf[first // PAIR][:, first % PAIR * PACK : (first % PAIR + count) * PACK]

        def gelu(c):
            nc.scalar.activation(
                out=h_values(c * CHUNK, CHUNK).rearrange("p (n t) -> p n t", t=PACK),
                in_=h_ps[c][:].rearrange("p t n -> p n t"),
                func=GELU,
            )

        def quantise_h(first, count):
            cols = slice(first, first + count)
            values = h_values(first, count)
            nc.vector.quantize_mx(out=h_codes[:, cols].bitcast(FP8X4), scales=h_scale[:, cols], in_=values)

        def second_layer(bank, tiles, first, count):
            y_ps = psum.tile([P, len(tiles), count], F32, name=f"y_ps{tiles[0]}_{first}", tag=f"bank{bank}")
            cols = slice(first, first + count)
            for i, t in enumerate(tiles):
                m = slice(t * P, (t + 1) * P)
                nc.tensor.matmul_mx(
                    out=y_ps[:, i, :],
                    lhsT=w2_codes[:, m].bitcast(FP8X4),
                    lhsT_scale=w2_scale[:, m],
                    rhs=h_codes[:, cols].bitcast(FP8X4),
                    rhs_scale=h_scale[:, cols],
                    start=True,
                    stop=True,
                )
            return y_ps


        def place(t, first):
            if first == 0 and t in (B, D):
                first = PAIR
            return (A, B, D, C).index(t) * ROW + FIRST + first

        def y_of(t, first, count):
            return stage[:, place(t, first) : place(t, first) + count]

        def vector_scatter(t, first, count):
            nc.vector.tensor_copy(out=windows[t][:].indirect(picks(first, count)), in_=y_of(t, first, count))

        def scalar_scatter(t, first, count):
            nc.scalar.activation(out=windows[t][:].indirect(picks(first, count)), in_=y_of(t, first, count), func=COPY)

        deal(nc.scalar.copy, w2_codes[:].bitcast(U32), w2_word_raw[:].bitcast(U32))
        h_bf = [tile("h_early", [P, PAIR * PACK], BF16, tag="w2_word_raw")]
        for c in range(2):
            first_layer(c, 1, x_early[:, c, :])
            gelu(c)
        x_late = tile("x_late", [P, PAIR], U32)
        gather_words(x_late[:], 1, PAIR)
        w2_scale = tile("w2_scale", [P, N], U8)
        deal(nc.vector.tensor_copy, w2_scale[:], w2_scale_raw[:])
        h_codes = shared.tile([P, S], U32, name="h_codes", align_bytes=64, offset=0)
        h_bf.append(shared.tile([P, PAIR * PACK], BF16, name="h_late", align_bytes=64, offset=4 * S))
        quantise_h(0, CHUNK)
        ac0 = second_layer(4, (A, C), 0, CHUNK)
        bd0 = second_layer(0, (B, D), 0, CHUNK)
        for c in range(2):
            first_layer(2 + c, 1, x_late[:, c * CHUNK : (c + 1) * CHUNK])
            gelu(2 + c)
        quantise_h(CHUNK, CHUNK)
        a1 = second_layer(6, (A,), CHUNK, CHUNK)
        bdc1 = second_layer(5, (B, D, C), CHUNK, CHUNK)
        rows = stage[:, : PACK * ROW].rearrange("p (t c) -> p t c", t=PACK)
        nc.vector.tensor_copy(out=rows[:, ::3, FIRST : FIRST + CHUNK], in_=ac0[:])
        nc.vector.tensor_copy(out=rows[:, 1:3, FIRST + PAIR : FIRST + PAIR + CHUNK], in_=bd0[:])
        nc.vector.tensor_copy(out=y_of(A, CHUNK, CHUNK), in_=a1[:, 0, :])
        quantise_h(PAIR, PAIR)
        nc.scalar.copy(out=rows[:, 1:, FIRST + CHUNK : FIRST + PAIR], in_=bdc1[:])
        vector_scatter(A, 0, PAIR)
        ac2 = second_layer(4, (A, C), PAIR, PAIR)
        bd2 = second_layer(7, (B, D), PAIR, PAIR)
        scalar_scatter(B, 0, CHUNK)
        scalar_scatter(D, 0, CHUNK)
        nc.vector.tensor_copy(out=y_of(A, PAIR, PAIR), in_=ac2[:, 0, :])
        nc.vector.tensor_copy(out=y_of(C, PAIR, PAIR), in_=ac2[:, 1, :])
        nc.scalar.copy(out=y_of(B, PAIR, PAIR), in_=bd2[:, 0, :])
        nc.scalar.copy(out=y_of(D, PAIR, PAIR), in_=bd2[:, 1, :])

        pairs = stage[:].bitcast(BF16).rearrange("p (u c e) -> p u c e", u=2, e=2)[:, :, :T]
        pair_words = stage[:].rearrange("p (u c) -> p u c", u=2)[:, :, :T]
        rounded = tile("rounded", [P, T, PACK], BF16)
        rounded_words = rounded[:].rearrange("p c t -> p (c t)").bitcast(U32).rearrange("p (c u) -> p c u", u=2)

        def store(t):
            nc.sync.dma_start(out=out_rows[t], in_=windows[t][:])

        def pool_round(t, cols, one):
            nc.gpsimd.tensor_scalar(pairs[:, 0, cols, t], windows[t][:, cols], one, -0.0, mybir.AluOpType.mult, mybir.AluOpType.add)

        vector_scatter(A, PAIR, PAIR)
        store(A)
        pool_round(A, slice(0, T - CHUNK), one)
        scalar_scatter(B, CHUNK, S - CHUNK)
        store(B)
        pool_round(B, slice(PAIR, T - CHUNK), 1.0)
        vector_scatter(C, 0, S)
        store(C)
        nc.vector.tensor_copy(out=pairs[:, 0, :PAIR, B], in_=windows[B][:, :PAIR])
        nc.vector.tensor_copy(out=pairs[:, 1, :SPLIT_C, 0], in_=windows[C][:, :SPLIT_C])
        scalar_scatter(D, CHUNK, S - CHUNK)
        store(D)
        nc.scalar.activation(out=pairs[:, 1, SPLIT_C:, 0], in_=windows[C][:, SPLIT_C:], func=IDENTITY, bias=nothing)
        for t in (A, B):
            nc.scalar.copy(out=pairs[:, 0, T - CHUNK :, t], in_=windows[t][:, T - CHUNK :])

        out_codes = tile("out_codes", [P, T], I32)
        out_scale = tile("out_scale", [P, T], U8)
        out_words = out_1[0].rearrange("p c r -> p (c r)").bitcast(I32)

        def quantise_out(cols):
            nc.vector.quantize_mx(
                out=out_codes[:, cols].bitcast(FP8X4),
                scales=out_scale[:, cols],
                in_=rounded[:, cols, :].rearrange("p c t -> p (c t)"),
            )

        def weave(copy, dtype, cols):
            copy(out=rounded_words[:, cols, :].bitcast(dtype), in_=pair_words[:, :, cols].bitcast(dtype).rearrange("p u c -> p c u"))

        def store_words(cols):
            nc.sync.dma_start(out=out_words[:, cols], in_=out_codes[:, cols])

        first_cols, vector_cols = slice(0, PAIR), slice(PAIR, 5 * CHUNK)
        late_cols, last_cols = slice(5 * CHUNK, 7 * CHUNK), slice(7 * CHUNK, T)
        for cols in (first_cols, vector_cols, slice(5 * CHUNK, T)):
            nc.vector.tensor_copy(out=pairs[:, 1, cols, 1], in_=windows[D][:, cols])
        for cols in (first_cols, late_cols, last_cols):
            weave(nc.scalar.copy, U32, cols)
        weave(nc.vector.tensor_copy, I32, vector_cols)
        quantise_out(first_cols)
        store_words(first_cols)
        quantise_out(vector_cols)
        store_words(vector_cols)
        quantise_out(late_cols)
        quantise_out(last_cols)
        store_words(slice(5 * CHUNK, T))
        for q in range(QUADS):
            queue = nc.sync if q % 2 == 0 else nc.scalar
            queue.dma_start(
                out=out_2[0, 4 * q : 4 * q + 4, :].bitcast(I32),
                in_=out_scale[32 * q : 32 * q + 4, :].bitcast(I32),
            )
